import numpy as np
import ml_dtypes


def mxq(x, axis, fmt="e4m3"):
    dtype, down = {"e4m3": (ml_dtypes.float8_e4m3fn, 7), "e5m2": (ml_dtypes.float8_e5m2, 14)}[fmt]
    v = np.moveaxis(np.asarray(x, np.float32).astype(ml_dtypes.bfloat16).astype(np.float64), axis, -1)
    blocks = v.reshape(v.shape[:-1] + (-1, 32))
    amax = np.abs(blocks).max(-1, keepdims=True)
    byte = np.maximum(np.where(amax > 0, np.frexp(amax)[1] - 1 + 127, 0) - down, 1)
    scale = np.exp2(byte - 127.0)
    codes = (blocks / scale).astype(np.float32).astype(dtype).astype(np.float64)
    return np.moveaxis((codes * scale).reshape(v.shape), -1, axis)


WIDE = False


def mx_kscale(k):
    if not WIDE:
        return np.ones(k)
    levels = np.array([10, -10, 5, -5, 0])
    if k % 512:
        return np.exp2(np.random.permutation(np.resize(levels, k // 32))).repeat(32)
    a = np.empty((k // 512, 16))
    for p in range(k // 512):
        a[p, :8] = np.random.permutation(np.resize(levels, 8))
        for g in range(8):
            far = levels[np.abs(levels - a[p, g]) >= 10]
            a[p, g + 8] = far[np.random.randint(len(far))]
    return np.exp2(a.ravel()).repeat(32)


def f64(x):
    return np.asarray(x).astype(np.float64)


def striped(idx):
    return np.tile(np.asarray(idx).reshape(-1, 16).T, (8, 1)).astype(np.uint16)


def unstriped(offs):
    return offs[:16].T.reshape(-1).astype(np.int64)


E2M1 = np.array([0.0, 0.5, 1.0, 1.5, 2.0, 3.0, 4.0, 6.0, -0.0, -0.5, -1.0, -1.5, -2.0, -3.0, -4.0, -6.0])


def pack_weight(w, fmt):
    k, n = w.shape
    w = f64(np.asarray(w, np.float32).astype(ml_dtypes.bfloat16)).reshape(k // 32, 32, n)
    amax = np.abs(w).max(1)
    if fmt == "e4m3":
        byte = np.frexp(amax)[1] - 1 + 127 - 7
    else:
        mant, ex = np.frexp(amax / 6.0)
        byte = np.where(mant > 0.5, ex, ex - 1) + 127
    byte = np.clip(np.where(amax > 0, byte, 1), 1, 254)
    scaled = (w * np.exp2(127.0 - byte)[:, None, :]).reshape(k, n).astype(np.float32)
    by_word = np.ascontiguousarray(scaled.reshape(k // 512, 128, 4, n).transpose(0, 1, 3, 2))
    if fmt == "e4m3":
        words = by_word.astype(ml_dtypes.float8_e4m3fn).view(np.uint8)
    else:
        c = by_word.astype(ml_dtypes.float4_e2m1fn).view(np.uint8) & 0xF
        words = (c[..., 0::2] | (c[..., 1::2] << 4)).reshape(k // 512, 128, 2 * n)
    return np.ascontiguousarray(words), np.ascontiguousarray(byte.astype(np.uint8).reshape(k // 512, 16, n))


def unpack_weight(words, scales, fmt):
    g, _, n = scales.shape
    words = np.ascontiguousarray(words).reshape(g, 128, n, -1)
    if fmt == "e4m3":
        vals = words.view(ml_dtypes.float8_e4m3fn).astype(np.float64)
    else:
        nib = np.empty((g, 128, n, 4), np.uint8)
        nib[..., 0::2] = words & 0xF
        nib[..., 1::2] = words >> 4
        vals = E2M1[nib]
    vals = vals * np.repeat(np.exp2(scales.astype(np.float64) - 127.0), 8, axis=1)[..., None]
    return vals.transpose(0, 1, 3, 2).reshape(g * 512, n)


B, N, T, D, DV, NQ = 1, 1024, 4096, 1024, 128, 128
PAGE = 512


def setup_inputs():
    n = np.random.standard_normal
    pages = np.random.permutation(T // PAGE)[:B * N // PAGE]
    idx = (pages[:, None] * PAGE + np.arange(PAGE)[None, :]).reshape(-1)
    s = mx_kscale(D)[:, None]
    u = np.ones(T)
    u[idx] = mx_kscale(B * N)
    r = np.random.uniform(0.5, 2.0, T)
    qp = [pack_weight(x, "e4m3") for x in n((B, D, NQ)) * s * (0.80 / np.sqrt(D))]
    k = n((D, T)) / s
    v = n((DV, T)) / (u * r)
    kp = pack_weight(k, "e2m1")
    vp = pack_weight(v.T, "e4m3")
    return {
        "q_words": np.stack([x[0] for x in qp]),
        "q_scales": np.stack([x[1] for x in qp]),
        "k_words": np.ascontiguousarray(kp[0].reshape(D // 1024, 2, 128, T, 2).transpose(0, 2, 3, 1, 4)).reshape(D // 1024, 128, T, 4),
        "k_scales": kp[1],
        "v_words": vp[0],
        "v_scales": vp[1],
        "vs": np.tile(u * r, (128, 1)).astype(np.float32),
        "og": n((B, NQ, DV)).astype(np.float32),
        "offs": striped(idx),
        "voffs": striped((pages[:, None] * DV + np.arange(DV)[None, :]).reshape(-1)),
    }


def reference(q_words, q_scales, k_words, k_scales, v_words, v_scales, vs, og, offs, voffs):
    idx = unstriped(offs)
    k = unpack_weight(k_words.reshape(D // 1024, 128, T, 2, 2).transpose(0, 3, 1, 2, 4).reshape(D // 512, 128, 2 * T), k_scales, "e2m1")
    v = unpack_weight(v_words, v_scales, "e4m3")
    v = v.reshape(T // 512, 512, DV)[unstriped(voffs)[::DV] // DV].reshape(B, N, DV)
    pick = lambda x: x[:, idx].reshape(x.shape[0], B, N).transpose(1, 0, 2)
    q = np.stack([unpack_weight(q_words[b], q_scales[b], "e4m3") for b in range(B)])
    score = q.transpose(0, 2, 1) @ pick(k)
    p = 1.0 / (1.0 + np.exp(-score))
    w = p * pick(f64(vs))[:, :1, :]
    y = mxq(w, 2, "e4m3") @ v
    y = y / 16.0
    y = y / (1.0 + np.exp(-f64(og)))
    return y

@@ -1,0 +1,171 @@
+from contextlib import ExitStack
+
+import concourse.mybir as mybir
+from concourse.masks import make_identity
+
+N, T, D, DV, NQ = 1024, 4096, 1024, 128, 128
+P = 128
+PAGE = 512
+PAGES = N // PAGE
+PASSES = D // 512
+POOL_PAGES = T // PAGE
+HALF = NQ // 2
+
+FLOPS = 2 * NQ * N * (D + DV)
+BYTES = P * T * 4 + 32 * T + POOL_PAGES * (P * DV * 4 + 16 * DV) + PASSES * (P * NQ * 4 + 16 * NQ) + T * 4 + 2 * NQ * DV * 4 + P * (N + PAGES * DV) // 8
+
+F32 = mybir.dt.float32
+BF16 = mybir.dt.bfloat16
+I32 = mybir.dt.int32
+U32 = mybir.dt.uint32
+U16 = mybir.dt.uint16
+U8 = mybir.dt.uint8
+FP8X4 = mybir.dt.float8_e4m3fn_x4
+FP4X4 = mybir.dt.float4_e2m1fn_x4
+MULT = mybir.AluOpType.mult
+SIGMOID = mybir.ActivationFunctionType.Sigmoid
+
+
+def tile_attend_pkv4q_sigm_gate_kernel(
+    tc, q_words, q_scales, k_words, k_scales, v_words, v_scales, vs, og, offs, voffs, out
+):
+    nc = tc.nc
+    with ExitStack() as ctx:
+        lists = ctx.enter_context(tc.tile_pool(name="lists", bufs=1))
+        held = ctx.enter_context(tc.tile_pool(name="held", bufs=1))
+        shared = ctx.enter_context(tc.tile_pool(name="shared", bufs=1))
+        psum = ctx.enter_context(tc.psum_pool(name="psum", bufs=1))
+
+        def own(shape, dtype, name):
+            return held.tile(shape, dtype, name=name, align_bytes=64)
+
+        def at(offset, shape, dtype, name):
+            return shared.tile(shape, dtype, name=name, align_bytes=64, offset=offset)
+
+        slots = lists.tile([P, N // 16], U16, name="slots")
+        vcols = lists.tile([P, PAGES * DV // 16], U16, name="vcols")
+        nc.sync.dma_start(slots[:], offs)
+        nc.sync.dma_start(vcols[:], voffs)
+
+        k_pool = own([P, T], U32, "k_pool")
+        nc.sync.dma_start(k_pool[:].bitcast(I32), k_words[0].rearrange("p t b -> p (t b)").bitcast(I32))
+
+        vs_pool = at(9216, [P, T], F32, "vs_pool")
+        nc.gpsimd.dma_start(vs_pool[P - 1 : P, :], vs[0:1, :])
+
+        ks_pool = at(0, [P, T], U8, "ks_pool")
+        nc.vector.memset(ks_pool[:].bitcast(I32), 0)
+        for r in range(4):
+            nc.scalar.dma_start(ks_pool[r:P:32, :].bitcast(I32), k_scales[0, r:16:4, :].bitcast(I32))
+        nc.scalar.dma_start(ks_pool[4:P:8, :].bitcast(I32), k_scales[1].bitcast(I32))
+
+        q_plane = own([P, PASSES, NQ], U8, "q_plane")
+        nc.vector.memset(q_plane[:].bitcast(I32), 0)
+        for r in range(4):
+            nc.gpsimd.dma_start(
+                q_plane[r:P:32, :, :].bitcast(I32), q_scales[0, :, r:16:4, :].rearrange("o f q -> f o q").bitcast(I32)
+            )
+        ident = own([P, P], F32, "ident")
+        make_identity(nc, ident[:])
+
+        k_plane1 = own([P, N], U8, "k_plane1")
+        nc.vector.memset(k_plane1[:].bitcast(I32), 0)
+        nc.vector.memset(vs_pool[0 : P - 1, :], 0.0)
+
+        vsc_pool = own([P, POOL_PAGES * DV], U8, "vsc_pool")
+        nc.vector.memset(vsc_pool[:].bitcast(I32), 0)
+        for r in range(4):
+            nc.sync.dma_start(
+                vsc_pool[r:P:32, :].bitcast(I32).rearrange("f (u e) -> f u e", u=POOL_PAGES),
+                v_scales[:, r:16:4, :].rearrange("u f e -> f u e").bitcast(I32),
+            )
+
+        ks_got = at(4608, [P, N], U8, "ks_got")
+        nc.vector.tensor_copy(ks_got[:], ks_pool[:].indirect(slots[:]))
+        k_plane0 = own([P, N], U8, "k_plane0")
+        nc.vector.tensor_copy(
+            k_plane0[:].rearrange("p (c t m) -> p c t m", c=PAGES, t=4),
+            ks_got[:].rearrange("p (c m t) -> p c t m", c=PAGES, t=4),
+        )
+        for r in range(4):
+            nc.scalar.dma_start(k_plane1[r:P:32, :].bitcast(I32), k_plane0[8 * r + 4 : P : 32, :].bitcast(I32))
+        k_planes = (k_plane0, k_plane1)
+
+        v_pool = at(0, [P, POOL_PAGES * DV], U32, "v_pool")
+        nc.sync.dma_start(
+            v_pool[:].bitcast(I32).rearrange("p (u e) -> p u e", u=POOL_PAGES),
+            v_words.rearrange("u p e r -> p u (e r)").bitcast(I32),
+        )
+        q_codes = at(4096, [P, PASSES, NQ], U32, "q_codes")
+        nc.scalar.dma_start(q_codes[:].bitcast(I32), q_words[0].rearrange("o p q r -> p o (q r)").bitcast(I32))
+
+        vs_got = at(5120, [P, N], F32, "vs_got")
+        vs_t = [psum.tile([P, 4, P], F32, name=f"vs_t{c}") for c in range(PAGES)]
+        for c in range(PAGES):
+            cols = slice(c * PAGE, (c + 1) * PAGE)
+            nc.vector.tensor_copy(vs_got[:, cols], vs_pool[:].indirect(slots[:, c * 32 : (c + 1) * 32]))
+            for t in range(4):
+                nc.tensor.transpose(vs_t[c][:, t, :], vs_got[:, c * PAGE + t : (c + 1) * PAGE : 4], ident[:])
+
+        og_sb = at(9216, [P, DV], F32, "og_sb")
+        nc.sync.dma_start(og_sb[:], og[0])
+
+        k_got = [at(10240 + 2048 * c, [P, PAGE], U32, f"k_got{c}") for c in range(PAGES)]
+        for c in range(PAGES):
+            nc.vector.tensor_copy(k_got[c][:], k_pool[:].indirect(slots[:, c * 32 : (c + 1) * 32]))
+        scores = [psum.tile([P, 4, NQ], F32, name=f"scores{c}") for c in range(PAGES)]
+        for c in range(PAGES):
+            k_codes = own([P, PASSES, 2 * PAGE], U8, f"k_codes{c}")
+            dst = k_codes[:].bitcast(U16).rearrange("p o (t m) -> p o m t", t=4)
+            src = k_got[c][:].bitcast(U16).rearrange("p (m t o) -> p o m t", t=4, o=PASSES)
+            for a in range(2):
+                nc.vector.tensor_copy(dst[:, :, :, 2 * a : 2 * a + 2], src[:, :, :, 2 * a : 2 * a + 2])
+                for t in range(2 * a, 2 * a + 2):
+                    for o in range(PASSES):
+                        nc.tensor.matmul_mx(
+                            out=scores[c][:, t, :],
+                            lhsT=k_codes[:, o, 256 * t : 256 * (t + 1)].bitcast(FP4X4),
+                            lhsT_scale=k_planes[o][:, c * PAGE + P * t : c * PAGE + P * (t + 1)],
+                            rhs=q_codes[:, o, :].bitcast(FP8X4),
+                            rhs_scale=q_plane[:, o, :],
+                            start=(o == 0),
+                            stop=(o == PASSES - 1),
+                        )
+
+        v_got = at(10240 + 2048, [P, PAGES * DV], U32, "v_got")
+        nc.vector.tensor_copy(v_got[:], v_pool[:].indirect(vcols[:]))
+        v_plane = at(10240 + 3072, [P, PAGES * DV], U8, "v_plane")
+        nc.vector.tensor_copy(v_plane[:], vsc_pool[:].indirect(vcols[:]))
+
+        acc = psum.tile([NQ, DV], F32, name="acc")
+        for c in range(PAGES):
+            prob = at(25600 + 2048 * c, [P, NQ, 4], F32, f"prob{c}")
+            w = own([P, NQ, 4], BF16, f"w{c}")
+            w_codes = own([P, NQ], U32, f"w_codes{c}")
+            w_plane = own([P, NQ], U8, f"w_plane{c}")
+            factor = vs_t[c][:, :, P - 1 : P].rearrange("p t o -> p o t").to_broadcast([P, HALF, 4])
+            halves = [slice(h * HALF, (h + 1) * HALF) for h in range(2)]
+            for qs in halves:
+                nc.scalar.activation(prob[:, qs, :], scores[c][:, :, qs].rearrange("p t q -> p q t"), SIGMOID)
+                nc.vector.tensor_tensor(w[:, qs, :], prob[:, qs, :], factor, MULT)
+            for qs in halves:
+                nc.vector.quantize_mx(
+                    out=w_codes[:, qs].bitcast(FP8X4),
+                    scales=w_plane[:, qs],
+                    in_=w[:, qs, :].rearrange("p q t -> p (q t)"),
+                )
+            nc.tensor.matmul_mx(
+                out=acc[:],
+                lhsT=w_codes[:].bitcast(FP8X4),
+                lhsT_scale=w_plane[:],
+                rhs=v_got[:, c * DV : (c + 1) * DV].bitcast(FP8X4),
+                rhs_scale=v_plane[:, c * DV : (c + 1) * DV],
+                start=(c == 0),
+                stop=(c == PAGES - 1),
+            )
+
+        gate = at(25600, [NQ, DV], F32, "gate")
+        nc.scalar.activation(gate[:], og_sb[:], SIGMOID)
+        result = own([NQ, DV], F32, "result")
+        nc.vector.scalar_tensor_tensor(result[:], acc[:], 1.0 / 16.0, gate[:], MULT, MULT)
+        nc.sync.dma_start(out[0], result[:])

@@ -42,22 +42,23 @@ def tile_attend_pkv4q_sigm_gate_kernel(
         def at(offset, shape, dtype, name):
             return shared.tile(shape, dtype, name=name, align_bytes=64, offset=offset)
 
+        ident = own([P, P], F32, "ident")
+        make_identity(nc, ident[:])
+
         slots = lists.tile([P, N // 16], U16, name="slots")
         vcols = lists.tile([P, PAGES * DV // 16], U16, name="vcols")
-        nc.sync.dma_start(slots[:], offs)
-        nc.sync.dma_start(vcols[:], voffs)
-
+        ks_pool = own([P, T], U8, "ks_pool")
+        vs_pool = at(8192, [P, T], F32, "vs_pool")
+        og_sb = own([P, DV], F32, "og_sb")
         k_pool = own([P, T], U32, "k_pool")
+        q_codes = own([P, PASSES, NQ], U32, "q_codes")
+        nc.scalar.dma_start(vs_pool[P - 1 : P, :], vs[0:1, :])
+        nc.sync.dma_start(slots[:], offs)
+        nc.sync.dma_start(og_sb[:], og[0])
+        nc.sync.dma_start(vcols[:], voffs)
+        nc.sync.dma_start(ks_pool[96:P, :].bitcast(I32), k_scales.rearrange("o f t -> (o f) t").bitcast(I32))
         nc.sync.dma_start(k_pool[:].bitcast(I32), k_words[0].rearrange("p t b -> p (t b)").bitcast(I32))
-
-        vs_pool = at(9216, [P, T], F32, "vs_pool")
-        nc.gpsimd.dma_start(vs_pool[P - 1 : P, :], vs[0:1, :])
-
-        ks_pool = at(0, [P, T], U8, "ks_pool")
-        nc.vector.memset(ks_pool[:].bitcast(I32), 0)
-        for r in range(4):
-            nc.scalar.dma_start(ks_pool[r:P:32, :].bitcast(I32), k_scales[0, r:16:4, :].bitcast(I32))
-        nc.scalar.dma_start(ks_pool[4:P:8, :].bitcast(I32), k_scales[1].bitcast(I32))
+        nc.sync.dma_start(q_codes[:].bitcast(I32), q_words[0].rearrange("o p q r -> p o (q r)").bitcast(I32))
 
         q_plane = own([P, PASSES, NQ], U8, "q_plane")
         nc.vector.memset(q_plane[:].bitcast(I32), 0)
@@ -65,55 +66,54 @@ def tile_attend_pkv4q_sigm_gate_kernel(
             nc.gpsimd.dma_start(
                 q_plane[r:P:32, :, :].bitcast(I32), q_scales[0, :, r:16:4, :].rearrange("o f q -> f o q").bitcast(I32)
             )
-        ident = own([P, P], F32, "ident")
-        make_identity(nc, ident[:])
-
-        k_plane1 = own([P, N], U8, "k_plane1")
-        nc.vector.memset(k_plane1[:].bitcast(I32), 0)
+        nc.vector.memset(ks_pool[0:96, :].bitcast(I32), 0)
+        k_plane = own([P, PASSES, N], U8, "k_plane")
+        nc.vector.memset(k_plane[:].bitcast(I32), 0)
         nc.vector.memset(vs_pool[0 : P - 1, :], 0.0)
 
-        vsc_pool = own([P, POOL_PAGES * DV], U8, "vsc_pool")
+        gate = own([NQ, DV], F32, "gate")
+        nc.scalar.activation(gate[:], og_sb[:], SIGMOID)
+
+        ks_got = at(0, [P, N], U8, "ks_got")
+        nc.vector.tensor_copy(ks_got[:], ks_pool[:].indirect(slots[:]))
+        ks_turned = own([P, N], U8, "ks_turned")
+        nc.vector.tensor_copy(
+            ks_turned[:].rearrange("p (c t m) -> p c t m", c=PAGES, t=4),
+            ks_got[:].rearrange("p (c m t) -> p c t m", c=PAGES, t=4),
+        )
+        for o in range(PASSES):
+            for r in range(4):
+                queue = nc.gpsimd if r == 0 else nc.scalar
+                first = 96 + 16 * o + r
+                queue.dma_start(k_plane[r:P:32, o, :].bitcast(I32), ks_turned[first : 112 + 16 * o : 4, :].bitcast(I32))
+
+        vs_got = at(0, [P, N], F32, "vs_got")
+        vs_col = own([P, PAGES, 4], F32, "vs_col")
+        for c in range(PAGES):
+            cols = slice(c * PAGE, (c + 1) * PAGE)
+            nc.vector.tensor_copy(vs_got[:, cols], vs_pool[:].indirect(slots[:, c * 32 : (c + 1) * 32]))
+            vs_t = psum.tile([P, 4, P], F32, name=f"vs_t{c}", tag=f"bank{c}")
+            for t in range(4):
+                nc.tensor.transpose(vs_t[:, t, :], vs_got[:, c * PAGE + t : (c + 1) * PAGE : 4], ident[:])
+            nc.scalar.copy(vs_col[:, c, :], vs_t[:, :, P - 1])
+
+        vsc_pool = at(8192, [P, POOL_PAGES * DV], U8, "vsc_pool")
         nc.vector.memset(vsc_pool[:].bitcast(I32), 0)
         for r in range(4):
             nc.sync.dma_start(
                 vsc_pool[r:P:32, :].bitcast(I32).rearrange("f (u e) -> f u e", u=POOL_PAGES),
                 v_scales[:, r:16:4, :].rearrange("u f e -> f u e").bitcast(I32),
             )
-
-        ks_got = at(4608, [P, N], U8, "ks_got")
-        nc.vector.tensor_copy(ks_got[:], ks_pool[:].indirect(slots[:]))
-        k_plane0 = own([P, N], U8, "k_plane0")
-        nc.vector.tensor_copy(
-            k_plane0[:].rearrange("p (c t m) -> p c t m", c=PAGES, t=4),
-            ks_got[:].rearrange("p (c m t) -> p c t m", c=PAGES, t=4),
-        )
-        for r in range(4):
-            nc.scalar.dma_start(k_plane1[r:P:32, :].bitcast(I32), k_plane0[8 * r + 4 : P : 32, :].bitcast(I32))
-        k_planes = (k_plane0, k_plane1)
-
-        v_pool = at(0, [P, POOL_PAGES * DV], U32, "v_pool")
+        v_pool = at(16384, [P, POOL_PAGES * DV], U32, "v_pool")
         nc.sync.dma_start(
             v_pool[:].bitcast(I32).rearrange("p (u e) -> p u e", u=POOL_PAGES),
             v_words.rearrange("u p e r -> p u (e r)").bitcast(I32),
         )
-        q_codes = at(4096, [P, PASSES, NQ], U32, "q_codes")
-        nc.scalar.dma_start(q_codes[:].bitcast(I32), q_words[0].rearrange("o p q r -> p o (q r)").bitcast(I32))
-
-        vs_got = at(5120, [P, N], F32, "vs_got")
-        vs_t = [psum.tile([P, 4, P], F32, name=f"vs_t{c}") for c in range(PAGES)]
-        for c in range(PAGES):
-            cols = slice(c * PAGE, (c + 1) * PAGE)
-            nc.vector.tensor_copy(vs_got[:, cols], vs_pool[:].indirect(slots[:, c * 32 : (c + 1) * 32]))
-            for t in range(4):
-                nc.tensor.transpose(vs_t[c][:, t, :], vs_got[:, c * PAGE + t : (c + 1) * PAGE : 4], ident[:])
-
-        og_sb = at(9216, [P, DV], F32, "og_sb")
-        nc.sync.dma_start(og_sb[:], og[0])
 
         k_got = [at(10240 + 2048 * c, [P, PAGE], U32, f"k_got{c}") for c in range(PAGES)]
         for c in range(PAGES):
             nc.vector.tensor_copy(k_got[c][:], k_pool[:].indirect(slots[:, c * 32 : (c + 1) * 32]))
-        scores = [psum.tile([P, 4, NQ], F32, name=f"scores{c}") for c in range(PAGES)]
+        scores = [psum.tile([P, 4, NQ], F32, name=f"scores{c}", tag=f"bank{c}") for c in range(PAGES)]
         for c in range(PAGES):
             k_codes = own([P, PASSES, 2 * PAGE], U8, f"k_codes{c}")
             dst = k_codes[:].bitcast(U16).rearrange("p o (t m) -> p o m t", t=4)
@@ -125,7 +125,7 @@ def tile_attend_pkv4q_sigm_gate_kernel(
                         nc.tensor.matmul_mx(
                             out=scores[c][:, t, :],
                             lhsT=k_codes[:, o, 256 * t : 256 * (t + 1)].bitcast(FP4X4),
-                            lhsT_scale=k_planes[o][:, c * PAGE + P * t : c * PAGE + P * (t + 1)],
+                            lhsT_scale=k_plane[:, o, c * PAGE + P * t : c * PAGE + P * (t + 1)],
                             rhs=q_codes[:, o, :].bitcast(FP8X4),
                             rhs_scale=q_plane[:, o, :],
                             start=(o == 0),
@@ -139,11 +139,11 @@ def tile_attend_pkv4q_sigm_gate_kernel(
 
         acc = psum.tile([NQ, DV], F32, name="acc")
         for c in range(PAGES):
-            prob = at(25600 + 2048 * c, [P, NQ, 4], F32, f"prob{c}")
+            prob = own([P, NQ, 4], F32, f"prob{c}")
             w = own([P, NQ, 4], BF16, f"w{c}")
             w_codes = own([P, NQ], U32, f"w_codes{c}")
             w_plane = own([P, NQ], U8, f"w_plane{c}")
-            factor = vs_t[c][:, :, P - 1 : P].rearrange("p t o -> p o t").to_broadcast([P, HALF, 4])
+            factor = vs_col[:, c : c + 1, :].to_broadcast([P, HALF, 4])
             halves = [slice(h * HALF, (h + 1) * HALF) for h in range(2)]
             for qs in halves:
                 nc.scalar.activation(prob[:, qs, :], scores[c][:, :, qs].rearrange("p t q -> p q t"), SIGMOID)
@@ -164,8 +164,6 @@ def tile_attend_pkv4q_sigm_gate_kernel(
                 stop=(c == PAGES - 1),
             )
 
-        gate = at(25600, [NQ, DV], F32, "gate")
-        nc.scalar.activation(gate[:], og_sb[:], SIGMOID)
         result = own([NQ, DV], F32, "result")
         nc.vector.scalar_tensor_tensor(result[:], acc[:], 1.0 / 16.0, gate[:], MULT, MULT)
         nc.sync.dma_start(out[0], result[:])

@@ -10,6 +10,7 @@ PAGES = N // PAGE
 PASSES = D // 512
 POOL_PAGES = T // PAGE
 HALF = NQ // 2
+SPLIT = 2816
 
 FLOPS = 2 * NQ * N * (D + DV)
 BYTES = P * T * 4 + 32 * T + POOL_PAGES * (P * DV * 4 + 16 * DV) + PASSES * (P * NQ * 4 + 16 * NQ) + T * 4 + 2 * NQ * DV * 4 + P * (N + PAGES * DV) // 8
@@ -49,14 +50,16 @@ def tile_attend_pkv4q_sigm_gate_kernel(
         vcols = lists.tile([P, PAGES * DV // 16], U16, name="vcols")
         ks_pool = own([P, T], U8, "ks_pool")
         vs_pool = at(8192, [P, T], F32, "vs_pool")
+        vs_head = own([P, 8], F32, "vs_head")
         og_sb = own([P, DV], F32, "og_sb")
         k_pool = own([P, T], U32, "k_pool")
         q_codes = own([P, PASSES, NQ], U32, "q_codes")
         nc.scalar.dma_start(vs_pool[P - 1 : P, :], vs[0:1, :])
+        nc.sync.dma_start(ks_pool[96:P, :].bitcast(I32), k_scales.rearrange("o f t -> (o f) t").bitcast(I32))
         nc.sync.dma_start(slots[:], offs)
         nc.sync.dma_start(og_sb[:], og[0])
+        nc.sync.dma_start(vs_head[:], vs[:, 0:8])
         nc.sync.dma_start(vcols[:], voffs)
-        nc.sync.dma_start(ks_pool[96:P, :].bitcast(I32), k_scales.rearrange("o f t -> (o f) t").bitcast(I32))
         nc.sync.dma_start(k_pool[:].bitcast(I32), k_words[0].rearrange("p t b -> p (t b)").bitcast(I32))
         nc.sync.dma_start(q_codes[:].bitcast(I32), q_words[0].rearrange("o p q r -> p o (q r)").bitcast(I32))
 
@@ -69,10 +72,11 @@ def tile_attend_pkv4q_sigm_gate_kernel(
         nc.vector.memset(ks_pool[0:96, :].bitcast(I32), 0)
         k_plane = own([P, PASSES, N], U8, "k_plane")
         nc.vector.memset(k_plane[:].bitcast(I32), 0)
-        nc.vector.memset(vs_pool[0 : P - 1, :], 0.0)
+        nc.vector.memset(vs_pool[0 : P - 1, 0:SPLIT], 0.0)
 
         gate = own([NQ, DV], F32, "gate")
         nc.scalar.activation(gate[:], og_sb[:], SIGMOID)
+        nc.scalar.copy(vs_pool[0 : P - 1, SPLIT:T], vs_head[0 : P - 1, 0:1].to_broadcast([P - 1, T - SPLIT]))
 
         ks_got = at(0, [P, N], U8, "ks_got")
         nc.vector.tensor_copy(ks_got[:], ks_pool[:].indirect(slots[:]))
@@ -83,9 +87,8 @@ def tile_attend_pkv4q_sigm_gate_kernel(
         )
         for o in range(PASSES):
             for r in range(4):
-                queue = nc.gpsimd if r == 0 else nc.scalar
                 first = 96 + 16 * o + r
-                queue.dma_start(k_plane[r:P:32, o, :].bitcast(I32), ks_turned[first : 112 + 16 * o : 4, :].bitcast(I32))
+                nc.scalar.dma_start(k_plane[r:P:32, o, :].bitcast(I32), ks_turned[first : 112 + 16 * o : 4, :].bitcast(I32))
 
         vs_got = at(0, [P, N], F32, "vs_got")
         vs_col = own([P, PAGES, 4], F32, "vs_col")

@@ -10,7 +10,7 @@ PAGES = N // PAGE
 PASSES = D // 512
 POOL_PAGES = T // PAGE
 HALF = NQ // 2
-SPLIT = 2816
+SPLIT = 2304
 
 FLOPS = 2 * NQ * N * (D + DV)
 BYTES = P * T * 4 + 32 * T + POOL_PAGES * (P * DV * 4 + 16 * DV) + PASSES * (P * NQ * 4 + 16 * NQ) + T * 4 + 2 * NQ * DV * 4 + P * (N + PAGES * DV) // 8
@@ -54,14 +54,20 @@ def tile_attend_pkv4q_sigm_gate_kernel(
         og_sb = own([P, DV], F32, "og_sb")
         k_pool = own([P, T], U32, "k_pool")
         q_codes = own([P, PASSES, NQ], U32, "q_codes")
+        nc.sync.dma_start(ks_pool[0:32, :].bitcast(I32), k_scales.rearrange("o f t -> (o f) t").bitcast(I32))
+        nc.scalar.dma_start(og_sb[:], og[0])
+        nc.scalar.dma_start(vs_head[:], vs[:, 0:8])
         nc.scalar.dma_start(vs_pool[P - 1 : P, :], vs[0:1, :])
-        nc.sync.dma_start(ks_pool[96:P, :].bitcast(I32), k_scales.rearrange("o f t -> (o f) t").bitcast(I32))
         nc.sync.dma_start(slots[:], offs)
-        nc.sync.dma_start(og_sb[:], og[0])
-        nc.sync.dma_start(vs_head[:], vs[:, 0:8])
         nc.sync.dma_start(vcols[:], voffs)
         nc.sync.dma_start(k_pool[:].bitcast(I32), k_words[0].rearrange("p t b -> p (t b)").bitcast(I32))
         nc.sync.dma_start(q_codes[:].bitcast(I32), q_words[0].rearrange("o p q r -> p o (q r)").bitcast(I32))
+
+        v_pool = own([P, POOL_PAGES * DV], U32, "v_pool")
+        nc.sync.dma_start(
+            v_pool[:].bitcast(I32).rearrange("p (u e) -> p u e", u=POOL_PAGES),
+            v_words.rearrange("u p e r -> p u (e r)").bitcast(I32),
+        )
 
         q_plane = own([P, PASSES, NQ], U8, "q_plane")
         nc.vector.memset(q_plane[:].bitcast(I32), 0)
@@ -69,9 +75,17 @@ def tile_attend_pkv4q_sigm_gate_kernel(
             nc.gpsimd.dma_start(
                 q_plane[r:P:32, :, :].bitcast(I32), q_scales[0, :, r:16:4, :].rearrange("o f q -> f o q").bitcast(I32)
             )
-        nc.vector.memset(ks_pool[0:96, :].bitcast(I32), 0)
-        k_plane = own([P, PASSES, N], U8, "k_plane")
-        nc.vector.memset(k_plane[:].bitcast(I32), 0)
+        vsc_pool = own([P, POOL_PAGES * DV], U8, "vsc_pool")
+        nc.vector.memset(vsc_pool[:].bitcast(I32), 0)
+        for r in range(4):
+            nc.gpsimd.dma_start(
+                vsc_pool[r:P:32, :].bitcast(I32).rearrange("f (u e) -> f u e", u=POOL_PAGES),
+                v_scales[:, r:16:4, :].rearrange("u f e -> f u e").bitcast(I32),
+            )
+        nc.vector.memset(ks_pool[32:64, :].bitcast(I32), 0)
+        nc.vector.memset(ks_pool[64:P, :].bitcast(I32), 0)
+        k_plane1 = own([P, N], U8, "k_plane1")
+        nc.vector.memset(k_plane1[:].bitcast(I32), 0)
         nc.vector.memset(vs_pool[0 : P - 1, 0:SPLIT], 0.0)
 
         gate = own([NQ, DV], F32, "gate")
@@ -80,15 +94,18 @@ def tile_attend_pkv4q_sigm_gate_kernel(
 
         ks_got = at(0, [P, N], U8, "ks_got")
         nc.vector.tensor_copy(ks_got[:], ks_pool[:].indirect(slots[:]))
-        ks_turned = own([P, N], U8, "ks_turned")
+        k_plane0 = own([P, N], U8, "k_plane0")
         nc.vector.tensor_copy(
-            ks_turned[:].rearrange("p (c t m) -> p c t m", c=PAGES, t=4),
+            k_plane0[:].rearrange("p (c t m) -> p c t m", c=PAGES, t=4),
             ks_got[:].rearrange("p (c m t) -> p c t m", c=PAGES, t=4),
         )
-        for o in range(PASSES):
-            for r in range(4):
-                first = 96 + 16 * o + r
-                nc.scalar.dma_start(k_plane[r:P:32, o, :].bitcast(I32), ks_turned[first : 112 + 16 * o : 4, :].bitcast(I32))
+        for quad in range(1, 4):
+            nc.scalar.dma_start(
+                k_plane0[32 * quad : 32 * quad + 4, :].bitcast(I32), k_plane0[4 * quad : 4 * quad + 4, :].bitcast(I32)
+            )
+        for r in range(4):
+            nc.scalar.dma_start(k_plane1[r:P:32, :].bitcast(I32), k_plane0[16 + r : 32 : 4, :].bitcast(I32))
+        k_planes = (k_plane0, k_plane1)
 
         vs_got = at(0, [P, N], F32, "vs_got")
         vs_col = own([P, PAGES, 4], F32, "vs_col")
@@ -99,19 +116,6 @@ def tile_attend_pkv4q_sigm_gate_kernel(
             for t in range(4):
                 nc.tensor.transpose(vs_t[:, t, :], vs_got[:, c * PAGE + t : (c + 1) * PAGE : 4], ident[:])
             nc.scalar.copy(vs_col[:, c, :], vs_t[:, :, P - 1])
-
-        vsc_pool = at(8192, [P, POOL_PAGES * DV], U8, "vsc_pool")
-        nc.vector.memset(vsc_pool[:].bitcast(I32), 0)
-        for r in range(4):
-            nc.sync.dma_start(
-                vsc_pool[r:P:32, :].bitcast(I32).rearrange("f (u e) -> f u e", u=POOL_PAGES),
-                v_scales[:, r:16:4, :].rearrange("u f e -> f u e").bitcast(I32),
-            )
-        v_pool = at(16384, [P, POOL_PAGES * DV], U32, "v_pool")
-        nc.sync.dma_start(
-            v_pool[:].bitcast(I32).rearrange("p (u e) -> p u e", u=POOL_PAGES),
-            v_words.rearrange("u p e r -> p u (e r)").bitcast(I32),
-        )
 
         k_got = [at(10240 + 2048 * c, [P, PAGE], U32, f"k_got{c}") for c in range(PAGES)]
         for c in range(PAGES):
@@ -128,7 +132,7 @@ def tile_attend_pkv4q_sigm_gate_kernel(
                         nc.tensor.matmul_mx(
                             out=scores[c][:, t, :],
                             lhsT=k_codes[:, o, 256 * t : 256 * (t + 1)].bitcast(FP4X4),
-                            lhsT_scale=k_plane[:, o, c * PAGE + P * t : c * PAGE + P * (t + 1)],
+                            lhsT_scale=k_planes[o][:, c * PAGE + P * t : c * PAGE + P * (t + 1)],
                             rhs=q_codes[:, o, :].bitcast(FP8X4),
                             rhs_scale=q_plane[:, o, :],
                             start=(o == 0),

@@ -10,7 +10,7 @@ PAGES = N // PAGE
 PASSES = D // 512
 POOL_PAGES = T // PAGE
 HALF = NQ // 2
-SPLIT = 2304
+SPLIT = 1664
 
 FLOPS = 2 * NQ * N * (D + DV)
 BYTES = P * T * 4 + 32 * T + POOL_PAGES * (P * DV * 4 + 16 * DV) + PASSES * (P * NQ * 4 + 16 * NQ) + T * 4 + 2 * NQ * DV * 4 + P * (N + PAGES * DV) // 8
@@ -75,13 +75,6 @@ def tile_attend_pkv4q_sigm_gate_kernel(
             nc.gpsimd.dma_start(
                 q_plane[r:P:32, :, :].bitcast(I32), q_scales[0, :, r:16:4, :].rearrange("o f q -> f o q").bitcast(I32)
             )
-        vsc_pool = own([P, POOL_PAGES * DV], U8, "vsc_pool")
-        nc.vector.memset(vsc_pool[:].bitcast(I32), 0)
-        for r in range(4):
-            nc.gpsimd.dma_start(
-                vsc_pool[r:P:32, :].bitcast(I32).rearrange("f (u e) -> f u e", u=POOL_PAGES),
-                v_scales[:, r:16:4, :].rearrange("u f e -> f u e").bitcast(I32),
-            )
         nc.vector.memset(ks_pool[32:64, :].bitcast(I32), 0)
         nc.vector.memset(ks_pool[64:P, :].bitcast(I32), 0)
         k_plane1 = own([P, N], U8, "k_plane1")
@@ -112,26 +105,34 @@ def tile_attend_pkv4q_sigm_gate_kernel(
         for c in range(PAGES):
             cols = slice(c * PAGE, (c + 1) * PAGE)
             nc.vector.tensor_copy(vs_got[:, cols], vs_pool[:].indirect(slots[:, c * 32 : (c + 1) * 32]))
-            vs_t = psum.tile([P, 4, P], F32, name=f"vs_t{c}", tag=f"bank{c}")
+            vs_t = psum.tile([P, 4, P], F32, name=f"vs_t{c}", tag=f"bank{2 * c}")
             for t in range(4):
                 nc.tensor.transpose(vs_t[:, t, :], vs_got[:, c * PAGE + t : (c + 1) * PAGE : 4], ident[:])
             nc.scalar.copy(vs_col[:, c, :], vs_t[:, :, P - 1])
 
+        vsc_pool = at(8192, [P, POOL_PAGES * DV], U8, "vsc_pool")
+        nc.gpsimd.memset(vsc_pool[:].bitcast(I32), 0)
+        for r in range(4):
+            nc.sync.dma_start(
+                vsc_pool[r:P:32, :].bitcast(I32).rearrange("f (u e) -> f u e", u=POOL_PAGES),
+                v_scales[:, r:16:4, :].rearrange("u f e -> f u e").bitcast(I32),
+            )
+
         k_got = [at(10240 + 2048 * c, [P, PAGE], U32, f"k_got{c}") for c in range(PAGES)]
         for c in range(PAGES):
             nc.vector.tensor_copy(k_got[c][:], k_pool[:].indirect(slots[:, c * 32 : (c + 1) * 32]))
-        scores = [psum.tile([P, 4, NQ], F32, name=f"scores{c}", tag=f"bank{c}") for c in range(PAGES)]
+        scores = [psum.tile([P, 2, NQ], F32, name=f"scores{b}", tag=f"bank{b}") for b in range(2 * PAGES)]
         for c in range(PAGES):
-            k_codes = own([P, PASSES, 2 * PAGE], U8, f"k_codes{c}")
-            dst = k_codes[:].bitcast(U16).rearrange("p o (t m) -> p o m t", t=4)
             src = k_got[c][:].bitcast(U16).rearrange("p (m t o) -> p o m t", t=4, o=PASSES)
             for a in range(2):
-                nc.vector.tensor_copy(dst[:, :, :, 2 * a : 2 * a + 2], src[:, :, :, 2 * a : 2 * a + 2])
+                k_codes = own([P, PASSES, PAGE], U8, f"k_codes{c}{a}")
+                dst = k_codes[:].bitcast(U16).rearrange("p o (t m) -> p o m t", t=2)
+                nc.vector.tensor_copy(dst, src[:, :, :, 2 * a : 2 * a + 2])
                 for t in range(2 * a, 2 * a + 2):
                     for o in range(PASSES):
                         nc.tensor.matmul_mx(
-                            out=scores[c][:, t, :],
-                            lhsT=k_codes[:, o, 256 * t : 256 * (t + 1)].bitcast(FP4X4),
+                            out=scores[2 * c + a][:, t % 2, :],
+                            lhsT=k_codes[:, o, 256 * (t % 2) : 256 * (t % 2 + 1)].bitcast(FP4X4),
                             lhsT_scale=k_planes[o][:, c * PAGE + P * t : c * PAGE + P * (t + 1)],
                             rhs=q_codes[:, o, :].bitcast(FP8X4),
                             rhs_scale=q_plane[:, o, :],
@@ -146,15 +147,21 @@ def tile_attend_pkv4q_sigm_gate_kernel(
 
         acc = psum.tile([NQ, DV], F32, name="acc")
         for c in range(PAGES):
-            prob = own([P, NQ, 4], F32, f"prob{c}")
+            prob = own([P, 2, NQ, 2], F32, f"prob{c}")
             w = own([P, NQ, 4], BF16, f"w{c}")
             w_codes = own([P, NQ], U32, f"w_codes{c}")
             w_plane = own([P, NQ], U8, f"w_plane{c}")
-            factor = vs_col[:, c : c + 1, :].to_broadcast([P, HALF, 4])
+            factor = vs_col[:, c : c + 1, :].rearrange("p o (a t) -> p o a t", a=2).to_broadcast([P, HALF, 2, 2])
             halves = [slice(h * HALF, (h + 1) * HALF) for h in range(2)]
+            nc.scalar.activation(prob[:, 0, :, :], scores[2 * c][:].rearrange("p t q -> p q t"), SIGMOID)
             for qs in halves:
-                nc.scalar.activation(prob[:, qs, :], scores[c][:, :, qs].rearrange("p t q -> p q t"), SIGMOID)
-                nc.vector.tensor_tensor(w[:, qs, :], prob[:, qs, :], factor, MULT)
+                nc.scalar.activation(prob[:, 1, qs, :], scores[2 * c + 1][:, :, qs].rearrange("p t q -> p q t"), SIGMOID)
+                nc.vector.tensor_tensor(
+                    w[:, qs, :].rearrange("p q (a t) -> p q a t", a=2),
+                    prob[:, :, qs, :].rearrange("p a q t -> p q a t"),
+                    factor,
+                    MULT,
+                )
             for qs in halves:
                 nc.vector.quantize_mx(
                     out=w_codes[:, qs].bitcast(FP8X4),

@@ -1,7 +1,6 @@
 from contextlib import ExitStack
 
 import concourse.mybir as mybir
-from concourse.masks import make_identity
 
 N, T, D, DV, NQ = 1024, 4096, 1024, 128, 128
 P = 128
@@ -10,7 +9,7 @@ PAGES = N // PAGE
 PASSES = D // 512
 POOL_PAGES = T // PAGE
 HALF = NQ // 2
-SPLIT = 1664
+SPLIT = 1280
 
 FLOPS = 2 * NQ * N * (D + DV)
 BYTES = P * T * 4 + 32 * T + POOL_PAGES * (P * DV * 4 + 16 * DV) + PASSES * (P * NQ * 4 + 16 * NQ) + T * 4 + 2 * NQ * DV * 4 + P * (N + PAGES * DV) // 8
@@ -43,43 +42,37 @@ def tile_attend_pkv4q_sigm_gate_kernel(
         def at(offset, shape, dtype, name):
             return shared.tile(shape, dtype, name=name, align_bytes=64, offset=offset)
 
-        ident = own([P, P], F32, "ident")
-        make_identity(nc, ident[:])
-
         slots = lists.tile([P, N // 16], U16, name="slots")
         vcols = lists.tile([P, PAGES * DV // 16], U16, name="vcols")
         ks_pool = own([P, T], U8, "ks_pool")
-        vs_pool = at(8192, [P, T], F32, "vs_pool")
+        vs_pool = own([P, T], F32, "vs_pool")
         vs_head = own([P, 8], F32, "vs_head")
         og_sb = own([P, DV], F32, "og_sb")
         k_pool = own([P, T], U32, "k_pool")
         q_codes = own([P, PASSES, NQ], U32, "q_codes")
+        planes = [own([P, N + NQ], U8, f"plane{o}") for o in range(PASSES)]
+        v_pool = own([P, POOL_PAGES * DV], U32, "v_pool")
+
         nc.sync.dma_start(ks_pool[0:32, :].bitcast(I32), k_scales.rearrange("o f t -> (o f) t").bitcast(I32))
+        nc.sync.dma_start(slots[:], offs)
         nc.scalar.dma_start(og_sb[:], og[0])
         nc.scalar.dma_start(vs_head[:], vs[:, 0:8])
-        nc.scalar.dma_start(vs_pool[P - 1 : P, :], vs[0:1, :])
-        nc.sync.dma_start(slots[:], offs)
-        nc.sync.dma_start(vcols[:], voffs)
+        nc.scalar.dma_start(planes[0][0:32, N:].bitcast(I32), q_scales[0].rearrange("o f q -> (o f) q").bitcast(I32))
+        nc.scalar.dma_start(q_codes[:].bitcast(I32), q_words[0].rearrange("o p q r -> p o (q r)").bitcast(I32))
+        nc.sync.dma_start(vs_pool[P - 1 : P, :], vs[0:1, :])
         nc.sync.dma_start(k_pool[:].bitcast(I32), k_words[0].rearrange("p t b -> p (t b)").bitcast(I32))
-        nc.sync.dma_start(q_codes[:].bitcast(I32), q_words[0].rearrange("o p q r -> p o (q r)").bitcast(I32))
-
-        v_pool = own([P, POOL_PAGES * DV], U32, "v_pool")
         nc.sync.dma_start(
             v_pool[:].bitcast(I32).rearrange("p (u e) -> p u e", u=POOL_PAGES),
             v_words.rearrange("u p e r -> p u (e r)").bitcast(I32),
         )
+        nc.sync.dma_start(vcols[:], voffs)
 
-        q_plane = own([P, PASSES, NQ], U8, "q_plane")
-        nc.vector.memset(q_plane[:].bitcast(I32), 0)
-        for r in range(4):
-            nc.gpsimd.dma_start(
-                q_plane[r:P:32, :, :].bitcast(I32), q_scales[0, :, r:16:4, :].rearrange("o f q -> f o q").bitcast(I32)
-            )
-        nc.vector.memset(ks_pool[32:64, :].bitcast(I32), 0)
+        nc.gpsimd.memset(ks_pool[32:64, :].bitcast(I32), 0)
         nc.vector.memset(ks_pool[64:P, :].bitcast(I32), 0)
-        k_plane1 = own([P, N], U8, "k_plane1")
-        nc.vector.memset(k_plane1[:].bitcast(I32), 0)
         nc.vector.memset(vs_pool[0 : P - 1, 0:SPLIT], 0.0)
+        nc.gpsimd.memset(planes[0][32:64, N:].bitcast(I32), 0)
+        nc.gpsimd.memset(planes[0][64:P, N:].bitcast(I32), 0)
+        nc.gpsimd.memset(planes[1][:].bitcast(I32), 0)
 
         gate = own([NQ, DV], F32, "gate")
         nc.scalar.activation(gate[:], og_sb[:], SIGMOID)
@@ -87,38 +80,34 @@ def tile_attend_pkv4q_sigm_gate_kernel(
 
         ks_got = at(0, [P, N], U8, "ks_got")
         nc.vector.tensor_copy(ks_got[:], ks_pool[:].indirect(slots[:]))
-        k_plane0 = own([P, N], U8, "k_plane0")
         nc.vector.tensor_copy(
-            k_plane0[:].rearrange("p (c t m) -> p c t m", c=PAGES, t=4),
+            planes[0][:, 0:N].rearrange("p (c t m) -> p c t m", c=PAGES, t=4),
             ks_got[:].rearrange("p (c m t) -> p c t m", c=PAGES, t=4),
         )
         for quad in range(1, 4):
             nc.scalar.dma_start(
-                k_plane0[32 * quad : 32 * quad + 4, :].bitcast(I32), k_plane0[4 * quad : 4 * quad + 4, :].bitcast(I32)
+                planes[0][32 * quad : 32 * quad + 4, :].bitcast(I32), planes[0][4 * quad : 4 * quad + 4, :].bitcast(I32)
             )
         for r in range(4):
-            nc.scalar.dma_start(k_plane1[r:P:32, :].bitcast(I32), k_plane0[16 + r : 32 : 4, :].bitcast(I32))
-        k_planes = (k_plane0, k_plane1)
+            nc.scalar.dma_start(planes[1][r:P:32, :].bitcast(I32), planes[0][16 + r : 32 : 4, :].bitcast(I32))
 
-        vs_got = at(0, [P, N], F32, "vs_got")
-        vs_col = own([P, PAGES, 4], F32, "vs_col")
-        for c in range(PAGES):
-            cols = slice(c * PAGE, (c + 1) * PAGE)
-            nc.vector.tensor_copy(vs_got[:, cols], vs_pool[:].indirect(slots[:, c * 32 : (c + 1) * 32]))
-            vs_t = psum.tile([P, 4, P], F32, name=f"vs_t{c}", tag=f"bank{2 * c}")
-            for t in range(4):
-                nc.tensor.transpose(vs_t[:, t, :], vs_got[:, c * PAGE + t : (c + 1) * PAGE : 4], ident[:])
-            nc.scalar.copy(vs_col[:, c, :], vs_t[:, :, P - 1])
-
-        vsc_pool = at(8192, [P, POOL_PAGES * DV], U8, "vsc_pool")
+        vsc_pool = at(0, [P, POOL_PAGES * DV], U8, "vsc_pool")
         nc.gpsimd.memset(vsc_pool[:].bitcast(I32), 0)
         for r in range(4):
-            nc.sync.dma_start(
+            nc.scalar.dma_start(
                 vsc_pool[r:P:32, :].bitcast(I32).rearrange("f (u e) -> f u e", u=POOL_PAGES),
                 v_scales[:, r:16:4, :].rearrange("u f e -> f u e").bitcast(I32),
             )
 
-        k_got = [at(10240 + 2048 * c, [P, PAGE], U32, f"k_got{c}") for c in range(PAGES)]
+        vs_col = []
+        for c in range(PAGES):
+            vs_got = own([P, PAGE], F32, f"vs_got{c}")
+            nc.vector.tensor_copy(vs_got[:], vs_pool[:].indirect(slots[:, c * 32 : (c + 1) * 32]))
+            col = own([P, 4], F32, f"vs_col{c}")
+            nc.scalar.dma_start(col[:], vs_got[P - 1 : P, :].rearrange("p (m t) -> p m t", t=4))
+            vs_col.append(col)
+
+        k_got = [own([P, PAGE], U32, f"k_got{c}") for c in range(PAGES)]
         for c in range(PAGES):
             nc.vector.tensor_copy(k_got[c][:], k_pool[:].indirect(slots[:, c * 32 : (c + 1) * 32]))
         scores = [psum.tile([P, 2, NQ], F32, name=f"scores{b}", tag=f"bank{b}") for b in range(2 * PAGES)]
@@ -133,16 +122,16 @@ def tile_attend_pkv4q_sigm_gate_kernel(
                         nc.tensor.matmul_mx(
                             out=scores[2 * c + a][:, t % 2, :],
                             lhsT=k_codes[:, o, 256 * (t % 2) : 256 * (t % 2 + 1)].bitcast(FP4X4),
-                            lhsT_scale=k_planes[o][:, c * PAGE + P * t : c * PAGE + P * (t + 1)],
+                            lhsT_scale=planes[o][:, c * PAGE + P * t : c * PAGE + P * (t + 1)],
                             rhs=q_codes[:, o, :].bitcast(FP8X4),
-                            rhs_scale=q_plane[:, o, :],
+                            rhs_scale=planes[o][:, N:],
                             start=(o == 0),
                             stop=(o == PASSES - 1),
                         )
 
-        v_got = at(10240 + 2048, [P, PAGES * DV], U32, "v_got")
+        v_got = own([P, PAGES * DV], U32, "v_got")
         nc.vector.tensor_copy(v_got[:], v_pool[:].indirect(vcols[:]))
-        v_plane = at(10240 + 3072, [P, PAGES * DV], U8, "v_plane")
+        v_plane = own([P, PAGES * DV], U8, "v_plane")
         nc.vector.tensor_copy(v_plane[:], vsc_pool[:].indirect(vcols[:]))
 
         acc = psum.tile([NQ, DV], F32, name="acc")
@@ -151,7 +140,7 @@ def tile_attend_pkv4q_sigm_gate_kernel(
             w = own([P, NQ, 4], BF16, f"w{c}")
             w_codes = own([P, NQ], U32, f"w_codes{c}")
             w_plane = own([P, NQ], U8, f"w_plane{c}")
-            factor = vs_col[:, c : c + 1, :].rearrange("p o (a t) -> p o a t", a=2).to_broadcast([P, HALF, 2, 2])
+            factor = vs_col[c][:].rearrange("p (o a t) -> p o a t", o=1, a=2).to_broadcast([P, HALF, 2, 2])
             halves = [slice(h * HALF, (h + 1) * HALF) for h in range(2)]
             nc.scalar.activation(prob[:, 0, :, :], scores[2 * c][:].rearrange("p t q -> p q t"), SIGMOID)
             for qs in halves:

@@ -9,7 +9,8 @@ PAGES = N // PAGE
 PASSES = D // 512
 POOL_PAGES = T // PAGE
 HALF = NQ // 2
-SPLIT = 1280
+SPLIT = 896
+WARM = 17
 
 FLOPS = 2 * NQ * N * (D + DV)
 BYTES = P * T * 4 + 32 * T + POOL_PAGES * (P * DV * 4 + 16 * DV) + PASSES * (P * NQ * 4 + 16 * NQ) + T * 4 + 2 * NQ * DV * 4 + P * (N + PAGES * DV) // 8
@@ -33,14 +34,10 @@ def tile_attend_pkv4q_sigm_gate_kernel(
     with ExitStack() as ctx:
         lists = ctx.enter_context(tc.tile_pool(name="lists", bufs=1))
         held = ctx.enter_context(tc.tile_pool(name="held", bufs=1))
-        shared = ctx.enter_context(tc.tile_pool(name="shared", bufs=1))
         psum = ctx.enter_context(tc.psum_pool(name="psum", bufs=1))
 
         def own(shape, dtype, name):
             return held.tile(shape, dtype, name=name, align_bytes=64)
-
-        def at(offset, shape, dtype, name):
-            return shared.tile(shape, dtype, name=name, align_bytes=64, offset=offset)
 
         slots = lists.tile([P, N // 16], U16, name="slots")
         vcols = lists.tile([P, PAGES * DV // 16], U16, name="vcols")
@@ -50,62 +47,64 @@ def tile_attend_pkv4q_sigm_gate_kernel(
         og_sb = own([P, DV], F32, "og_sb")
         k_pool = own([P, T], U32, "k_pool")
         q_codes = own([P, PASSES, NQ], U32, "q_codes")
-        planes = [own([P, N + NQ], U8, f"plane{o}") for o in range(PASSES)]
+        planes = [own([P, N + NQ + PAGES * DV], U8, "plane0"), own([P, N + NQ], U8, "plane1")]
+        q_cols = slice(N, N + NQ)
+        vsc_pool = own([P, POOL_PAGES * DV], U8, "vsc_pool")
+        nc.vector.memset(vsc_pool[:].bitcast(I32), 0)
         v_pool = own([P, POOL_PAGES * DV], U32, "v_pool")
 
-        nc.sync.dma_start(ks_pool[0:32, :].bitcast(I32), k_scales.rearrange("o f t -> (o f) t").bitcast(I32))
         nc.sync.dma_start(slots[:], offs)
-        nc.scalar.dma_start(og_sb[:], og[0])
+        nc.sync.dma_start(ks_pool[0:32, :].bitcast(I32), k_scales.rearrange("o f t -> (o f) t").bitcast(I32))
+        nc.sync.dma_start(vcols[:], voffs)
         nc.scalar.dma_start(vs_head[:], vs[:, 0:8])
-        nc.scalar.dma_start(planes[0][0:32, N:].bitcast(I32), q_scales[0].rearrange("o f q -> (o f) q").bitcast(I32))
-        nc.scalar.dma_start(q_codes[:].bitcast(I32), q_words[0].rearrange("o p q r -> p o (q r)").bitcast(I32))
+        nc.scalar.dma_start(
+            vsc_pool[0:16, :].bitcast(I32).rearrange("f (u e) -> f u e", u=POOL_PAGES),
+            v_scales.rearrange("u f e -> f u e").bitcast(I32),
+        )
         nc.sync.dma_start(vs_pool[P - 1 : P, :], vs[0:1, :])
+        nc.sync.dma_start(planes[0][0:32, q_cols].bitcast(I32), q_scales[0].rearrange("o f q -> (o f) q").bitcast(I32))
         nc.sync.dma_start(k_pool[:].bitcast(I32), k_words[0].rearrange("p t b -> p (t b)").bitcast(I32))
+        nc.sync.dma_start(q_codes[:].bitcast(I32), q_words[0].rearrange("o p q r -> p o (q r)").bitcast(I32))
         nc.sync.dma_start(
             v_pool[:].bitcast(I32).rearrange("p (u e) -> p u e", u=POOL_PAGES),
             v_words.rearrange("u p e r -> p u (e r)").bitcast(I32),
         )
-        nc.sync.dma_start(vcols[:], voffs)
+        nc.sync.dma_start(og_sb[:], og[0])
 
-        nc.gpsimd.memset(ks_pool[32:64, :].bitcast(I32), 0)
+        nc.vector.memset(ks_pool[32:64, :].bitcast(I32), 0)
         nc.vector.memset(ks_pool[64:P, :].bitcast(I32), 0)
         nc.vector.memset(vs_pool[0 : P - 1, 0:SPLIT], 0.0)
-        nc.gpsimd.memset(planes[0][32:64, N:].bitcast(I32), 0)
-        nc.gpsimd.memset(planes[0][64:P, N:].bitcast(I32), 0)
-        nc.gpsimd.memset(planes[1][:].bitcast(I32), 0)
+        nc.vector.memset(planes[0][32:64, q_cols].bitcast(I32), 0)
+        nc.vector.memset(planes[0][64:P, q_cols].bitcast(I32), 0)
+        nc.vector.memset(planes[1][:].bitcast(I32), 0)
 
-        gate = own([NQ, DV], F32, "gate")
-        nc.scalar.activation(gate[:], og_sb[:], SIGMOID)
         nc.scalar.copy(vs_pool[0 : P - 1, SPLIT:T], vs_head[0 : P - 1, 0:1].to_broadcast([P - 1, T - SPLIT]))
 
-        ks_got = at(0, [P, N], U8, "ks_got")
+        ks_got = own([P, N], U8, "ks_got")
         nc.vector.tensor_copy(ks_got[:], ks_pool[:].indirect(slots[:]))
+        vsc_got = own([P, PAGES * DV], U8, "vsc_got")
+        nc.vector.tensor_copy(vsc_got[:], vsc_pool[:].indirect(vcols[:]))
         nc.vector.tensor_copy(
             planes[0][:, 0:N].rearrange("p (c t m) -> p c t m", c=PAGES, t=4),
             ks_got[:].rearrange("p (c m t) -> p c t m", c=PAGES, t=4),
         )
+        nc.vector.tensor_copy(planes[0][:, N + NQ :].bitcast(I32), vsc_got[:].bitcast(I32))
         for quad in range(1, 4):
             nc.scalar.dma_start(
                 planes[0][32 * quad : 32 * quad + 4, :].bitcast(I32), planes[0][4 * quad : 4 * quad + 4, :].bitcast(I32)
             )
         for r in range(4):
-            nc.scalar.dma_start(planes[1][r:P:32, :].bitcast(I32), planes[0][16 + r : 32 : 4, :].bitcast(I32))
+            nc.scalar.dma_start(planes[1][r:P:32, :].bitcast(I32), planes[0][16 + r : 32 : 4, 0 : N + NQ].bitcast(I32))
 
-        vsc_pool = at(0, [P, POOL_PAGES * DV], U8, "vsc_pool")
-        nc.gpsimd.memset(vsc_pool[:].bitcast(I32), 0)
-        for r in range(4):
-            nc.scalar.dma_start(
-                vsc_pool[r:P:32, :].bitcast(I32).rearrange("f (u e) -> f u e", u=POOL_PAGES),
-                v_scales[:, r:16:4, :].rearrange("u f e -> f u e").bitcast(I32),
-            )
-
-        vs_col = []
+        vs_got = own([P, N], F32, "vs_got")
+        nc.vector.tensor_copy(vs_got[:], vs_pool[:].indirect(slots[:]))
+        vs_col = [own([P, 4], F32, f"vs_col{c}") for c in range(PAGES)]
         for c in range(PAGES):
-            vs_got = own([P, PAGE], F32, f"vs_got{c}")
-            nc.vector.tensor_copy(vs_got[:], vs_pool[:].indirect(slots[:, c * 32 : (c + 1) * 32]))
-            col = own([P, 4], F32, f"vs_col{c}")
-            nc.scalar.dma_start(col[:], vs_got[P - 1 : P, :].rearrange("p (m t) -> p m t", t=4))
-            vs_col.append(col)
+            row = vs_got[P - 1 : P, c * PAGE : (c + 1) * PAGE]
+            nc.scalar.dma_start(vs_col[c][:], row.rearrange("p (m t) -> p m t", t=4))
+
+        gate = own([NQ, DV], F32, "gate")
+        nc.scalar.activation(gate[:], og_sb[:], SIGMOID)
 
         k_got = [own([P, PAGE], U32, f"k_got{c}") for c in range(PAGES)]
         for c in range(PAGES):
@@ -124,15 +123,13 @@ def tile_attend_pkv4q_sigm_gate_kernel(
                             lhsT=k_codes[:, o, 256 * (t % 2) : 256 * (t % 2 + 1)].bitcast(FP4X4),
                             lhsT_scale=planes[o][:, c * PAGE + P * t : c * PAGE + P * (t + 1)],
                             rhs=q_codes[:, o, :].bitcast(FP8X4),
-                            rhs_scale=planes[o][:, N:],
+                            rhs_scale=planes[o][:, q_cols],
                             start=(o == 0),
                             stop=(o == PASSES - 1),
                         )
 
         v_got = own([P, PAGES * DV], U32, "v_got")
         nc.vector.tensor_copy(v_got[:], v_pool[:].indirect(vcols[:]))
-        v_plane = own([P, PAGES * DV], U8, "v_plane")
-        nc.vector.tensor_copy(v_plane[:], vsc_pool[:].indirect(vcols[:]))
 
         acc = psum.tile([NQ, DV], F32, name="acc")
         for c in range(PAGES):
@@ -162,7 +159,7 @@ def tile_attend_pkv4q_sigm_gate_kernel(
                 lhsT=w_codes[:].bitcast(FP8X4),
                 lhsT_scale=w_plane[:],
                 rhs=v_got[:, c * DV : (c + 1) * DV].bitcast(FP8X4),
-                rhs_scale=v_plane[:, c * DV : (c + 1) * DV],
+                rhs_scale=planes[0][:, N + NQ + c * DV : N + NQ + (c + 1) * DV],
                 start=(c == 0),
                 stop=(c == PAGES - 1),
             )

@@ -34,6 +34,7 @@ def tile_attend_pkv4q_sigm_gate_kernel(
     with ExitStack() as ctx:
         lists = ctx.enter_context(tc.tile_pool(name="lists", bufs=1))
         held = ctx.enter_context(tc.tile_pool(name="held", bufs=1))
+        late = ctx.enter_context(tc.tile_pool(name="late", bufs=1))
         psum = ctx.enter_context(tc.psum_pool(name="psum", bufs=1))
 
         def own(shape, dtype, name):
@@ -62,14 +63,13 @@ def tile_attend_pkv4q_sigm_gate_kernel(
             v_scales.rearrange("u f e -> f u e").bitcast(I32),
         )
         nc.sync.dma_start(vs_pool[P - 1 : P, :], vs[0:1, :])
-        nc.sync.dma_start(planes[0][0:32, q_cols].bitcast(I32), q_scales[0].rearrange("o f q -> (o f) q").bitcast(I32))
+        nc.scalar.dma_start(planes[0][0:32, q_cols].bitcast(I32), q_scales[0].rearrange("o f q -> (o f) q").bitcast(I32))
         nc.sync.dma_start(k_pool[:].bitcast(I32), k_words[0].rearrange("p t b -> p (t b)").bitcast(I32))
         nc.sync.dma_start(q_codes[:].bitcast(I32), q_words[0].rearrange("o p q r -> p o (q r)").bitcast(I32))
         nc.sync.dma_start(
             v_pool[:].bitcast(I32).rearrange("p (u e) -> p u e", u=POOL_PAGES),
             v_words.rearrange("u p e r -> p u (e r)").bitcast(I32),
         )
-        nc.sync.dma_start(og_sb[:], og[0])
 
         nc.vector.memset(ks_pool[32:64, :].bitcast(I32), 0)
         nc.vector.memset(ks_pool[64:P, :].bitcast(I32), 0)
@@ -78,6 +78,8 @@ def tile_attend_pkv4q_sigm_gate_kernel(
         nc.vector.memset(planes[0][64:P, q_cols].bitcast(I32), 0)
         nc.vector.memset(planes[1][:].bitcast(I32), 0)
 
+        table = own([P, 1], F32, "table")
+        nc.scalar.activation(table[:], vs_head[:, 0:1], SIGMOID)
         nc.scalar.copy(vs_pool[0 : P - 1, SPLIT:T], vs_head[0 : P - 1, 0:1].to_broadcast([P - 1, T - SPLIT]))
 
         ks_got = own([P, N], U8, "ks_got")
@@ -90,21 +92,20 @@ def tile_attend_pkv4q_sigm_gate_kernel(
         )
         nc.vector.tensor_copy(planes[0][:, N + NQ :].bitcast(I32), vsc_got[:].bitcast(I32))
         for quad in range(1, 4):
-            nc.scalar.dma_start(
+            nc.sync.dma_start(
                 planes[0][32 * quad : 32 * quad + 4, :].bitcast(I32), planes[0][4 * quad : 4 * quad + 4, :].bitcast(I32)
             )
         for r in range(4):
-            nc.scalar.dma_start(planes[1][r:P:32, :].bitcast(I32), planes[0][16 + r : 32 : 4, 0 : N + NQ].bitcast(I32))
+            nc.sync.dma_start(planes[1][r:P:32, :].bitcast(I32), planes[0][16 + r : 32 : 4, 0 : N + NQ].bitcast(I32))
 
         vs_got = own([P, N], F32, "vs_got")
         nc.vector.tensor_copy(vs_got[:], vs_pool[:].indirect(slots[:]))
         vs_col = [own([P, 4], F32, f"vs_col{c}") for c in range(PAGES)]
         for c in range(PAGES):
             row = vs_got[P - 1 : P, c * PAGE : (c + 1) * PAGE]
-            nc.scalar.dma_start(vs_col[c][:], row.rearrange("p (m t) -> p m t", t=4))
+            nc.sync.dma_start(vs_col[c][:], row.rearrange("p (m t) -> p m t", t=4))
 
-        gate = own([NQ, DV], F32, "gate")
-        nc.scalar.activation(gate[:], og_sb[:], SIGMOID)
+        nc.sync.dma_start(og_sb[:], og[0])
 
         k_got = [own([P, PAGE], U32, f"k_got{c}") for c in range(PAGES)]
         for c in range(PAGES):
@@ -113,7 +114,9 @@ def tile_attend_pkv4q_sigm_gate_kernel(
         for c in range(PAGES):
             src = k_got[c][:].bitcast(U16).rearrange("p (m t o) -> p o m t", t=4, o=PASSES)
             for a in range(2):
-                k_codes = own([P, PASSES, PAGE], U8, f"k_codes{c}{a}")
+                k_codes = late.tile(
+                    [P, PASSES, PAGE], U8, name=f"k_codes{c}{a}", align_bytes=64, offset=1024 * (3 - 2 * c - a)
+                )
                 dst = k_codes[:].bitcast(U16).rearrange("p o (t m) -> p o m t", t=2)
                 nc.vector.tensor_copy(dst, src[:, :, :, 2 * a : 2 * a + 2])
                 for t in range(2 * a, 2 * a + 2):
@@ -164,6 +167,8 @@ def tile_attend_pkv4q_sigm_gate_kernel(
                 stop=(c == PAGES - 1),
             )
 
+        gate = late.tile([NQ, DV], F32, name="gate", align_bytes=64, offset=0)
+        nc.scalar.activation(gate[:], og_sb[:], SIGMOID)
         result = own([NQ, DV], F32, "result")
         nc.vector.scalar_tensor_tensor(result[:], acc[:], 1.0 / 16.0, gate[:], MULT, MULT)
         nc.sync.dma_start(out[0], result[:])

@@ -63,7 +63,7 @@ def tile_attend_pkv4q_sigm_gate_kernel(
             v_scales.rearrange("u f e -> f u e").bitcast(I32),
         )
         nc.sync.dma_start(vs_pool[P - 1 : P, :], vs[0:1, :])
-        nc.scalar.dma_start(planes[0][0:32, q_cols].bitcast(I32), q_scales[0].rearrange("o f q -> (o f) q").bitcast(I32))
+        nc.sync.dma_start(planes[0][0:32, q_cols].bitcast(I32), q_scales[0].rearrange("o f q -> (o f) q").bitcast(I32))
         nc.sync.dma_start(k_pool[:].bitcast(I32), k_words[0].rearrange("p t b -> p (t b)").bitcast(I32))
         nc.sync.dma_start(q_codes[:].bitcast(I32), q_words[0].rearrange("o p q r -> p o (q r)").bitcast(I32))
         nc.sync.dma_start(
@@ -92,20 +92,32 @@ def tile_attend_pkv4q_sigm_gate_kernel(
         )
         nc.vector.tensor_copy(planes[0][:, N + NQ :].bitcast(I32), vsc_got[:].bitcast(I32))
         for quad in range(1, 4):
-            nc.sync.dma_start(
+            nc.scalar.dma_start(
                 planes[0][32 * quad : 32 * quad + 4, :].bitcast(I32), planes[0][4 * quad : 4 * quad + 4, :].bitcast(I32)
             )
         for r in range(4):
-            nc.sync.dma_start(planes[1][r:P:32, :].bitcast(I32), planes[0][16 + r : 32 : 4, 0 : N + NQ].bitcast(I32))
+            nc.scalar.dma_start(planes[1][r:P:32, :].bitcast(I32), planes[0][16 + r : 32 : 4, 0 : N + NQ].bitcast(I32))
 
         vs_got = own([P, N], F32, "vs_got")
         nc.vector.tensor_copy(vs_got[:], vs_pool[:].indirect(slots[:]))
         vs_col = [own([P, 4], F32, f"vs_col{c}") for c in range(PAGES)]
         for c in range(PAGES):
             row = vs_got[P - 1 : P, c * PAGE : (c + 1) * PAGE]
-            nc.sync.dma_start(vs_col[c][:], row.rearrange("p (m t) -> p m t", t=4))
+            nc.scalar.dma_start(vs_col[c][:], row.rearrange("p (m t) -> p m t", t=4))
 
         nc.sync.dma_start(og_sb[:], og[0])
+
+        warm = psum.tile([32, 4, NQ], F32, name="warm")
+        for i in range(WARM):
+            nc.tensor.matmul_mx(
+                out=warm[:, i % 4, :],
+                lhsT=q_codes[:, 0, 0:32].bitcast(FP8X4),
+                lhsT_scale=planes[0][:, N : N + 32],
+                rhs=q_codes[:, 0, :].bitcast(FP8X4),
+                rhs_scale=planes[0][:, q_cols],
+                start=True,
+                stop=True,
+            )
 
         k_got = [own([P, PAGE], U32, f"k_got{c}") for c in range(PAGES)]
         for c in range(PAGES):

@@ -52,10 +52,11 @@ def tile_attend_pkv4q_sigm_gate_kernel(
         q_cols = slice(N, N + NQ)
         vsc_pool = own([P, POOL_PAGES * DV], U8, "vsc_pool")
         nc.vector.memset(vsc_pool[:].bitcast(I32), 0)
+        nc.vector.memset(planes[0][:, q_cols].bitcast(I32), 0)
         v_pool = own([P, POOL_PAGES * DV], U32, "v_pool")
 
-        nc.sync.dma_start(slots[:], offs)
         nc.sync.dma_start(ks_pool[0:32, :].bitcast(I32), k_scales.rearrange("o f t -> (o f) t").bitcast(I32))
+        nc.sync.dma_start(slots[:], offs)
         nc.sync.dma_start(vcols[:], voffs)
         nc.scalar.dma_start(vs_head[:], vs[:, 0:8])
         nc.scalar.dma_start(
@@ -74,8 +75,6 @@ def tile_attend_pkv4q_sigm_gate_kernel(
         nc.vector.memset(ks_pool[32:64, :].bitcast(I32), 0)
         nc.vector.memset(ks_pool[64:P, :].bitcast(I32), 0)
         nc.vector.memset(vs_pool[0 : P - 1, 0:SPLIT], 0.0)
-        nc.vector.memset(planes[0][32:64, q_cols].bitcast(I32), 0)
-        nc.vector.memset(planes[0][64:P, q_cols].bitcast(I32), 0)
         nc.vector.memset(planes[1][:].bitcast(I32), 0)
 
         table = own([P, 1], F32, "table")
@@ -147,27 +146,29 @@ def tile_attend_pkv4q_sigm_gate_kernel(
         nc.vector.tensor_copy(v_got[:], v_pool[:].indirect(vcols[:]))
 
         acc = psum.tile([NQ, DV], F32, name="acc")
+        halves = [slice(h * HALF, (h + 1) * HALF) for h in range(2)]
+        pieces = ([slice(0, NQ)], halves)
+        w = [own([P, NQ, 4], BF16, f"w{c}") for c in range(PAGES)]
         for c in range(PAGES):
             prob = own([P, 2, NQ, 2], F32, f"prob{c}")
-            w = own([P, NQ, 4], BF16, f"w{c}")
-            w_codes = own([P, NQ], U32, f"w_codes{c}")
-            w_plane = own([P, NQ], U8, f"w_plane{c}")
-            factor = vs_col[c][:].rearrange("p (o a t) -> p o a t", o=1, a=2).to_broadcast([P, HALF, 2, 2])
-            halves = [slice(h * HALF, (h + 1) * HALF) for h in range(2)]
             nc.scalar.activation(prob[:, 0, :, :], scores[2 * c][:].rearrange("p t q -> p q t"), SIGMOID)
-            for qs in halves:
+            for qs in pieces[c]:
                 nc.scalar.activation(prob[:, 1, qs, :], scores[2 * c + 1][:, :, qs].rearrange("p t q -> p q t"), SIGMOID)
+                factor = vs_col[c][:].rearrange("p (o a t) -> p o a t", o=1, a=2)
                 nc.vector.tensor_tensor(
-                    w[:, qs, :].rearrange("p q (a t) -> p q a t", a=2),
+                    w[c][:, qs, :].rearrange("p q (a t) -> p q a t", a=2),
                     prob[:, :, qs, :].rearrange("p a q t -> p q a t"),
-                    factor,
+                    factor.to_broadcast([P, qs.stop - qs.start, 2, 2]),
                     MULT,
                 )
-            for qs in halves:
+        for c in range(PAGES):
+            w_codes = own([P, NQ], U32, f"w_codes{c}")
+            w_plane = own([P, NQ], U8, f"w_plane{c}")
+            for qs in pieces[c]:
                 nc.vector.quantize_mx(
                     out=w_codes[:, qs].bitcast(FP8X4),
                     scales=w_plane[:, qs],
-                    in_=w[:, qs, :].rearrange("p q t -> p (q t)"),
+                    in_=w[c][:, qs, :].rearrange("p q t -> p (q t)"),
                 )
             nc.tensor.matmul_mx(
                 out=acc[:],

@@ -9,7 +9,7 @@ PAGES = N // PAGE
 PASSES = D // 512
 POOL_PAGES = T // PAGE
 HALF = NQ // 2
-SPLIT = 896
+SPLIT = 1792
 WARM = 17
 
 FLOPS = 2 * NQ * N * (D + DV)

@@ -9,7 +9,7 @@ PAGES = N // PAGE
 PASSES = D // 512
 POOL_PAGES = T // PAGE
 HALF = NQ // 2
-SPLIT = 1792
+SPLIT = 1280
 WARM = 17
 
 FLOPS = 2 * NQ * N * (D + DV)
@@ -55,9 +55,9 @@ def tile_attend_pkv4q_sigm_gate_kernel(
         nc.vector.memset(planes[0][:, q_cols].bitcast(I32), 0)
         v_pool = own([P, POOL_PAGES * DV], U32, "v_pool")
 
+        nc.sync.dma_start(vcols[:], voffs)
         nc.sync.dma_start(ks_pool[0:32, :].bitcast(I32), k_scales.rearrange("o f t -> (o f) t").bitcast(I32))
         nc.sync.dma_start(slots[:], offs)
-        nc.sync.dma_start(vcols[:], voffs)
         nc.scalar.dma_start(vs_head[:], vs[:, 0:8])
         nc.scalar.dma_start(
             vsc_pool[0:16, :].bitcast(I32).rearrange("f (u e) -> f u e", u=POOL_PAGES),
@@ -75,21 +75,21 @@ def tile_attend_pkv4q_sigm_gate_kernel(
         nc.vector.memset(ks_pool[32:64, :].bitcast(I32), 0)
         nc.vector.memset(ks_pool[64:P, :].bitcast(I32), 0)
         nc.vector.memset(vs_pool[0 : P - 1, 0:SPLIT], 0.0)
-        nc.vector.memset(planes[1][:].bitcast(I32), 0)
 
         table = own([P, 1], F32, "table")
         nc.scalar.activation(table[:], vs_head[:, 0:1], SIGMOID)
         nc.scalar.copy(vs_pool[0 : P - 1, SPLIT:T], vs_head[0 : P - 1, 0:1].to_broadcast([P - 1, T - SPLIT]))
 
-        ks_got = own([P, N], U8, "ks_got")
-        nc.vector.tensor_copy(ks_got[:], ks_pool[:].indirect(slots[:]))
         vsc_got = own([P, PAGES * DV], U8, "vsc_got")
         nc.vector.tensor_copy(vsc_got[:], vsc_pool[:].indirect(vcols[:]))
+        ks_got = own([P, N], U8, "ks_got")
+        nc.vector.tensor_copy(ks_got[:], ks_pool[:].indirect(slots[:]))
+        nc.vector.tensor_copy(planes[0][:, N + NQ :].bitcast(I32), vsc_got[:].bitcast(I32))
+        nc.vector.memset(planes[1][:].bitcast(I32), 0)
         nc.vector.tensor_copy(
             planes[0][:, 0:N].rearrange("p (c t m) -> p c t m", c=PAGES, t=4),
             ks_got[:].rearrange("p (c m t) -> p c t m", c=PAGES, t=4),
         )
-        nc.vector.tensor_copy(planes[0][:, N + NQ :].bitcast(I32), vsc_got[:].bitcast(I32))
         for quad in range(1, 4):
             nc.scalar.dma_start(
                 planes[0][32 * quad : 32 * quad + 4, :].bitcast(I32), planes[0][4 * quad : 4 * quad + 4, :].bitcast(I32)

@@ -34,7 +34,6 @@ def tile_attend_pkv4q_sigm_gate_kernel(
     with ExitStack() as ctx:
         lists = ctx.enter_context(tc.tile_pool(name="lists", bufs=1))
         held = ctx.enter_context(tc.tile_pool(name="held", bufs=1))
-        late = ctx.enter_context(tc.tile_pool(name="late", bufs=1))
         psum = ctx.enter_context(tc.psum_pool(name="psum", bufs=1))
 
         def own(shape, dtype, name):
@@ -67,6 +66,7 @@ def tile_attend_pkv4q_sigm_gate_kernel(
         nc.sync.dma_start(planes[0][0:32, q_cols].bitcast(I32), q_scales[0].rearrange("o f q -> (o f) q").bitcast(I32))
         nc.sync.dma_start(k_pool[:].bitcast(I32), k_words[0].rearrange("p t b -> p (t b)").bitcast(I32))
         nc.sync.dma_start(q_codes[:].bitcast(I32), q_words[0].rearrange("o p q r -> p o (q r)").bitcast(I32))
+        nc.sync.dma_start(og_sb[:], og[0])
         nc.sync.dma_start(
             v_pool[:].bitcast(I32).rearrange("p (u e) -> p u e", u=POOL_PAGES),
             v_words.rearrange("u p e r -> p u (e r)").bitcast(I32),
@@ -76,8 +76,6 @@ def tile_attend_pkv4q_sigm_gate_kernel(
         nc.vector.memset(ks_pool[64:P, :].bitcast(I32), 0)
         nc.vector.memset(vs_pool[0 : P - 1, 0:SPLIT], 0.0)
 
-        table = own([P, 1], F32, "table")
-        nc.scalar.activation(table[:], vs_head[:, 0:1], SIGMOID)
         nc.scalar.copy(vs_pool[0 : P - 1, SPLIT:T], vs_head[0 : P - 1, 0:1].to_broadcast([P - 1, T - SPLIT]))
 
         vsc_got = own([P, PAGES * DV], U8, "vsc_got")
@@ -104,7 +102,8 @@ def tile_attend_pkv4q_sigm_gate_kernel(
             row = vs_got[P - 1 : P, c * PAGE : (c + 1) * PAGE]
             nc.scalar.dma_start(vs_col[c][:], row.rearrange("p (m t) -> p m t", t=4))
 
-        nc.sync.dma_start(og_sb[:], og[0])
+        gate = own([NQ, DV], F32, "gate")
+        nc.scalar.activation(gate[:], og_sb[:], SIGMOID)
 
         warm = psum.tile([32, 4, NQ], F32, name="warm")
         for i in range(WARM):
@@ -125,9 +124,7 @@ def tile_attend_pkv4q_sigm_gate_kernel(
         for c in range(PAGES):
             src = k_got[c][:].bitcast(U16).rearrange("p (m t o) -> p o m t", t=4, o=PASSES)
             for a in range(2):
-                k_codes = late.tile(
-                    [P, PASSES, PAGE], U8, name=f"k_codes{c}{a}", align_bytes=64, offset=1024 * (3 - 2 * c - a)
-                )
+                k_codes = own([P, PASSES, PAGE], U8, f"k_codes{c}{a}")
                 dst = k_codes[:].bitcast(U16).rearrange("p o (t m) -> p o m t", t=2)
                 nc.vector.tensor_copy(dst, src[:, :, :, 2 * a : 2 * a + 2])
                 for t in range(2 * a, 2 * a + 2):
@@ -152,7 +149,7 @@ def tile_attend_pkv4q_sigm_gate_kernel(
         for c in range(PAGES):
             prob = own([P, 2, NQ, 2], F32, f"prob{c}")
             nc.scalar.activation(prob[:, 0, :, :], scores[2 * c][:].rearrange("p t q -> p q t"), SIGMOID)
-            for qs in pieces[c]:
+            for qs in halves:
                 nc.scalar.activation(prob[:, 1, qs, :], scores[2 * c + 1][:, :, qs].rearrange("p t q -> p q t"), SIGMOID)
                 factor = vs_col[c][:].rearrange("p (o a t) -> p o a t", o=1, a=2)
                 nc.vector.tensor_tensor(
@@ -180,8 +177,6 @@ def tile_attend_pkv4q_sigm_gate_kernel(
                 stop=(c == PAGES - 1),
             )
 
-        gate = late.tile([NQ, DV], F32, name="gate", align_bytes=64, offset=0)
-        nc.scalar.activation(gate[:], og_sb[:], SIGMOID)
         result = own([NQ, DV], F32, "result")
         nc.vector.scalar_tensor_tensor(result[:], acc[:], 1.0 / 16.0, gate[:], MULT, MULT)
         nc.sync.dma_start(out[0], result[:])

@@ -9,8 +9,7 @@ PAGES = N // PAGE
 PASSES = D // 512
 POOL_PAGES = T // PAGE
 HALF = NQ // 2
-SPLIT = 1280
-WARM = 17
+SPLIT = 1024
 
 FLOPS = 2 * NQ * N * (D + DV)
 BYTES = P * T * 4 + 32 * T + POOL_PAGES * (P * DV * 4 + 16 * DV) + PASSES * (P * NQ * 4 + 16 * NQ) + T * 4 + 2 * NQ * DV * 4 + P * (N + PAGES * DV) // 8
@@ -34,48 +33,49 @@ def tile_attend_pkv4q_sigm_gate_kernel(
     with ExitStack() as ctx:
         lists = ctx.enter_context(tc.tile_pool(name="lists", bufs=1))
         held = ctx.enter_context(tc.tile_pool(name="held", bufs=1))
+        reused = ctx.enter_context(tc.tile_pool(name="reused", bufs=1))
         psum = ctx.enter_context(tc.psum_pool(name="psum", bufs=1))
 
         def own(shape, dtype, name):
             return held.tile(shape, dtype, name=name, align_bytes=64)
 
+        def reusing(shape, dtype, name, offset):
+            return reused.tile(shape, dtype, name=name, offset=offset, align_bytes=64)
+
         slots = lists.tile([P, N // 16], U16, name="slots")
         vcols = lists.tile([P, PAGES * DV // 16], U16, name="vcols")
         ks_pool = own([P, T], U8, "ks_pool")
-        vs_pool = own([P, T], F32, "vs_pool")
-        vs_head = own([P, 8], F32, "vs_head")
+        vs_pool = reusing([P, T], F32, "vs_pool", 0)
+        vs_head = reusing([P, 8], F32, "vs_head", 4 * T)
         og_sb = own([P, DV], F32, "og_sb")
         k_pool = own([P, T], U32, "k_pool")
         q_codes = own([P, PASSES, NQ], U32, "q_codes")
-        planes = [own([P, N + NQ + PAGES * DV], U8, "plane0"), own([P, N + NQ], U8, "plane1")]
+        planes = [own([P, N + NQ + PAGES * DV], U8, "plane0"), own([P, N + NQ + PAGES * DV], U8, "plane1")]
         q_cols = slice(N, N + NQ)
         vsc_pool = own([P, POOL_PAGES * DV], U8, "vsc_pool")
-        nc.vector.memset(vsc_pool[:].bitcast(I32), 0)
-        nc.vector.memset(planes[0][:, q_cols].bitcast(I32), 0)
-        v_pool = own([P, POOL_PAGES * DV], U32, "v_pool")
+        for rows in (slice(0, 16), slice(32, 64), slice(64, P)):
+            nc.vector.memset(vsc_pool[rows, :].bitcast(I32), 0)
+        nc.gpsimd.dma_start(og_sb[:], og[0])
+        nc.gpsimd.dma_start(q_codes[:].bitcast(I32), q_words[0].rearrange("o p q r -> p o (q r)").bitcast(I32))
 
-        nc.sync.dma_start(vcols[:], voffs)
-        nc.sync.dma_start(ks_pool[0:32, :].bitcast(I32), k_scales.rearrange("o f t -> (o f) t").bitcast(I32))
-        nc.sync.dma_start(slots[:], offs)
         nc.scalar.dma_start(vs_head[:], vs[:, 0:8])
-        nc.scalar.dma_start(
-            vsc_pool[0:16, :].bitcast(I32).rearrange("f (u e) -> f u e", u=POOL_PAGES),
+        nc.scalar.dma_start(planes[0][0:32, q_cols].bitcast(I32), q_scales[0].rearrange("o f q -> (o f) q").bitcast(I32))
+        nc.scalar.dma_start(vs_pool[P - 1 : P, :], vs[0:1, :])
+        nc.sync.dma_start(vcols[:], voffs)
+        nc.sync.dma_start(
+            vsc_pool[16:32, :].bitcast(I32).rearrange("f (u e) -> f u e", u=POOL_PAGES),
             v_scales.rearrange("u f e -> f u e").bitcast(I32),
         )
-        nc.sync.dma_start(vs_pool[P - 1 : P, :], vs[0:1, :])
-        nc.sync.dma_start(planes[0][0:32, q_cols].bitcast(I32), q_scales[0].rearrange("o f q -> (o f) q").bitcast(I32))
+        nc.sync.dma_start(ks_pool[0:32, :].bitcast(I32), k_scales.rearrange("o f t -> (o f) t").bitcast(I32))
+        nc.sync.dma_start(slots[:], offs)
         nc.sync.dma_start(k_pool[:].bitcast(I32), k_words[0].rearrange("p t b -> p (t b)").bitcast(I32))
-        nc.sync.dma_start(q_codes[:].bitcast(I32), q_words[0].rearrange("o p q r -> p o (q r)").bitcast(I32))
-        nc.sync.dma_start(og_sb[:], og[0])
-        nc.sync.dma_start(
-            v_pool[:].bitcast(I32).rearrange("p (u e) -> p u e", u=POOL_PAGES),
-            v_words.rearrange("u p e r -> p u (e r)").bitcast(I32),
-        )
 
         nc.vector.memset(ks_pool[32:64, :].bitcast(I32), 0)
         nc.vector.memset(ks_pool[64:P, :].bitcast(I32), 0)
         nc.vector.memset(vs_pool[0 : P - 1, 0:SPLIT], 0.0)
 
+        nc.vector.memset(planes[0][32:64, q_cols].bitcast(I32), 0)
+        nc.vector.memset(planes[0][64:P, q_cols].bitcast(I32), 0)
         nc.scalar.copy(vs_pool[0 : P - 1, SPLIT:T], vs_head[0 : P - 1, 0:1].to_broadcast([P - 1, T - SPLIT]))
 
         vsc_got = own([P, PAGES * DV], U8, "vsc_got")
@@ -90,53 +90,52 @@ def tile_attend_pkv4q_sigm_gate_kernel(
         )
         for quad in range(1, 4):
             nc.scalar.dma_start(
-                planes[0][32 * quad : 32 * quad + 4, :].bitcast(I32), planes[0][4 * quad : 4 * quad + 4, :].bitcast(I32)
+                planes[0][32 * quad : 32 * quad + 4, 0 : N + NQ].bitcast(I32),
+                planes[0][4 * quad : 4 * quad + 4, 0 : N + NQ].bitcast(I32),
             )
         for r in range(4):
-            nc.scalar.dma_start(planes[1][r:P:32, :].bitcast(I32), planes[0][16 + r : 32 : 4, 0 : N + NQ].bitcast(I32))
-
-        vs_got = own([P, N], F32, "vs_got")
-        nc.vector.tensor_copy(vs_got[:], vs_pool[:].indirect(slots[:]))
-        vs_col = [own([P, 4], F32, f"vs_col{c}") for c in range(PAGES)]
-        for c in range(PAGES):
-            row = vs_got[P - 1 : P, c * PAGE : (c + 1) * PAGE]
-            nc.scalar.dma_start(vs_col[c][:], row.rearrange("p (m t) -> p m t", t=4))
+            nc.scalar.dma_start(planes[1][r:P:32, :].bitcast(I32), planes[0][16 + r : 32 : 4, :].bitcast(I32))
 
         gate = own([NQ, DV], F32, "gate")
         nc.scalar.activation(gate[:], og_sb[:], SIGMOID)
 
-        warm = psum.tile([32, 4, NQ], F32, name="warm")
-        for i in range(WARM):
-            nc.tensor.matmul_mx(
-                out=warm[:, i % 4, :],
-                lhsT=q_codes[:, 0, 0:32].bitcast(FP8X4),
-                lhsT_scale=planes[0][:, N : N + 32],
-                rhs=q_codes[:, 0, :].bitcast(FP8X4),
-                rhs_scale=planes[0][:, q_cols],
-                start=True,
-                stop=True,
-            )
+        v_pool = own([P, POOL_PAGES * DV], U32, "v_pool")
+        nc.scalar.dma_start(
+            v_pool[:].bitcast(I32).rearrange("p (u e) -> p u e", u=POOL_PAGES),
+            v_words.rearrange("u p e r -> p u (e r)").bitcast(I32),
+        )
+        vs_col = [own([P, 4], F32, f"vs_col{c}") for c in range(PAGES)]
 
-        k_got = [own([P, PAGE], U32, f"k_got{c}") for c in range(PAGES)]
-        for c in range(PAGES):
-            nc.vector.tensor_copy(k_got[c][:], k_pool[:].indirect(slots[:, c * 32 : (c + 1) * 32]))
+        def page_slots(c):
+            return slots[:, c * 32 : (c + 1) * 32]
+
+        def gather_vs(c):
+            vs_got = own([P, PAGE], F32, f"vs_got{c}")
+            nc.vector.tensor_copy(vs_got[:], vs_pool[:].indirect(page_slots(c)))
+            nc.scalar.dma_start(vs_col[c][:], vs_got[P - 1 : P, :].rearrange("p (m t) -> p m t", t=4))
+
+        k_got = [reusing([P, PAGE], U32, f"k_got{c}", 4 * T * (1 - c)) for c in range(PAGES)]
         scores = [psum.tile([P, 2, NQ], F32, name=f"scores{b}", tag=f"bank{b}") for b in range(2 * PAGES)]
+        gather_vs(0)
         for c in range(PAGES):
+            nc.vector.tensor_copy(k_got[c][:], k_pool[:].indirect(page_slots(c)))
+            if c == 0:
+                gather_vs(1)
             src = k_got[c][:].bitcast(U16).rearrange("p (m t o) -> p o m t", t=4, o=PASSES)
             for a in range(2):
                 k_codes = own([P, PASSES, PAGE], U8, f"k_codes{c}{a}")
                 dst = k_codes[:].bitcast(U16).rearrange("p o (t m) -> p o m t", t=2)
                 nc.vector.tensor_copy(dst, src[:, :, :, 2 * a : 2 * a + 2])
                 for t in range(2 * a, 2 * a + 2):
-                    for o in range(PASSES):
+                    for o in reversed(range(PASSES)):
                         nc.tensor.matmul_mx(
                             out=scores[2 * c + a][:, t % 2, :],
                             lhsT=k_codes[:, o, 256 * (t % 2) : 256 * (t % 2 + 1)].bitcast(FP4X4),
                             lhsT_scale=planes[o][:, c * PAGE + P * t : c * PAGE + P * (t + 1)],
                             rhs=q_codes[:, o, :].bitcast(FP8X4),
                             rhs_scale=planes[o][:, q_cols],
-                            start=(o == 0),
-                            stop=(o == PASSES - 1),
+                            start=(o == PASSES - 1),
+                            stop=(o == 0),
                         )
 
         v_got = own([P, PAGES * DV], U32, "v_got")
@@ -172,7 +171,7 @@ def tile_attend_pkv4q_sigm_gate_kernel(
                 lhsT=w_codes[:].bitcast(FP8X4),
                 lhsT_scale=w_plane[:],
                 rhs=v_got[:, c * DV : (c + 1) * DV].bitcast(FP8X4),
-                rhs_scale=planes[0][:, N + NQ + c * DV : N + NQ + (c + 1) * DV],
+                rhs_scale=planes[1][:, N + NQ + c * DV : N + NQ + (c + 1) * DV],
                 start=(c == 0),
                 stop=(c == PAGES - 1),
             )

@@ -9,7 +9,7 @@ PAGES = N // PAGE
 PASSES = D // 512
 POOL_PAGES = T // PAGE
 HALF = NQ // 2
-SPLIT = 1024
+SPLIT = 768
 
 FLOPS = 2 * NQ * N * (D + DV)
 BYTES = P * T * 4 + 32 * T + POOL_PAGES * (P * DV * 4 + 16 * DV) + PASSES * (P * NQ * 4 + 16 * NQ) + T * 4 + 2 * NQ * DV * 4 + P * (N + PAGES * DV) // 8
@@ -36,8 +36,8 @@ def tile_attend_pkv4q_sigm_gate_kernel(
         reused = ctx.enter_context(tc.tile_pool(name="reused", bufs=1))
         psum = ctx.enter_context(tc.psum_pool(name="psum", bufs=1))
 
-        def own(shape, dtype, name):
-            return held.tile(shape, dtype, name=name, align_bytes=64)
+        def own(shape, dtype, name, tag=None):
+            return held.tile(shape, dtype, name=name, tag=tag or name, align_bytes=64)
 
         def reusing(shape, dtype, name, offset):
             return reused.tile(shape, dtype, name=name, offset=offset, align_bytes=64)
@@ -55,20 +55,25 @@ def tile_attend_pkv4q_sigm_gate_kernel(
         vsc_pool = own([P, POOL_PAGES * DV], U8, "vsc_pool")
         for rows in (slice(0, 16), slice(32, 64), slice(64, P)):
             nc.vector.memset(vsc_pool[rows, :].bitcast(I32), 0)
-        nc.gpsimd.dma_start(og_sb[:], og[0])
-        nc.gpsimd.dma_start(q_codes[:].bitcast(I32), q_words[0].rearrange("o p q r -> p o (q r)").bitcast(I32))
 
+        nc.scalar.dma_start(
+            vsc_pool[16:32, :].bitcast(I32).rearrange("f (u e) -> f u e", u=POOL_PAGES),
+            v_scales.rearrange("u f e -> f u e").bitcast(I32),
+        )
         nc.scalar.dma_start(vs_head[:], vs[:, 0:8])
         nc.scalar.dma_start(planes[0][0:32, q_cols].bitcast(I32), q_scales[0].rearrange("o f q -> (o f) q").bitcast(I32))
         nc.scalar.dma_start(vs_pool[P - 1 : P, :], vs[0:1, :])
         nc.sync.dma_start(vcols[:], voffs)
-        nc.sync.dma_start(
-            vsc_pool[16:32, :].bitcast(I32).rearrange("f (u e) -> f u e", u=POOL_PAGES),
-            v_scales.rearrange("u f e -> f u e").bitcast(I32),
-        )
         nc.sync.dma_start(ks_pool[0:32, :].bitcast(I32), k_scales.rearrange("o f t -> (o f) t").bitcast(I32))
         nc.sync.dma_start(slots[:], offs)
         nc.sync.dma_start(k_pool[:].bitcast(I32), k_words[0].rearrange("p t b -> p (t b)").bitcast(I32))
+        nc.sync.dma_start(q_codes[:].bitcast(I32), q_words[0].rearrange("o p q r -> p o (q r)").bitcast(I32))
+        nc.sync.dma_start(og_sb[:], og[0])
+        v_pool = own([P, POOL_PAGES * DV], U32, "v_pool")
+        nc.sync.dma_start(
+            v_pool[:].bitcast(I32).rearrange("p (u e) -> p u e", u=POOL_PAGES),
+            v_words.rearrange("u p e r -> p u (e r)").bitcast(I32),
+        )
 
         nc.vector.memset(ks_pool[32:64, :].bitcast(I32), 0)
         nc.vector.memset(ks_pool[64:P, :].bitcast(I32), 0)
@@ -99,11 +104,6 @@ def tile_attend_pkv4q_sigm_gate_kernel(
         gate = own([NQ, DV], F32, "gate")
         nc.scalar.activation(gate[:], og_sb[:], SIGMOID)
 
-        v_pool = own([P, POOL_PAGES * DV], U32, "v_pool")
-        nc.scalar.dma_start(
-            v_pool[:].bitcast(I32).rearrange("p (u e) -> p u e", u=POOL_PAGES),
-            v_words.rearrange("u p e r -> p u (e r)").bitcast(I32),
-        )
         vs_col = [own([P, 4], F32, f"vs_col{c}") for c in range(PAGES)]
 
         def page_slots(c):
@@ -138,7 +138,7 @@ def tile_attend_pkv4q_sigm_gate_kernel(
                             stop=(o == 0),
                         )
 
-        v_got = own([P, PAGES * DV], U32, "v_got")
+        v_got = own([P, PAGES * DV], U32, "v_got", "k_codes01")
         nc.vector.tensor_copy(v_got[:], v_pool[:].indirect(vcols[:]))
 
         acc = psum.tile([NQ, DV], F32, name="acc")

@@ -9,7 +9,7 @@ PAGES = N // PAGE
 PASSES = D // 512
 POOL_PAGES = T // PAGE
 HALF = NQ // 2
-SPLIT = 768
+SPLIT = 512
 
 FLOPS = 2 * NQ * N * (D + DV)
 BYTES = P * T * 4 + 32 * T + POOL_PAGES * (P * DV * 4 + 16 * DV) + PASSES * (P * NQ * 4 + 16 * NQ) + T * 4 + 2 * NQ * DV * 4 + P * (N + PAGES * DV) // 8
@@ -45,8 +45,8 @@ def tile_attend_pkv4q_sigm_gate_kernel(
         slots = lists.tile([P, N // 16], U16, name="slots")
         vcols = lists.tile([P, PAGES * DV // 16], U16, name="vcols")
         ks_pool = own([P, T], U8, "ks_pool")
-        vs_pool = reusing([P, T], F32, "vs_pool", 0)
-        vs_head = reusing([P, 8], F32, "vs_head", 4 * T)
+        vs_pool = own([P, T], F32, "vs_pool")
+        vs_head = reusing([P, 32], F32, "vs_head", 4 * PAGE - 64)
         og_sb = own([P, DV], F32, "og_sb")
         k_pool = own([P, T], U32, "k_pool")
         q_codes = own([P, PASSES, NQ], U32, "q_codes")
@@ -60,12 +60,12 @@ def tile_attend_pkv4q_sigm_gate_kernel(
             vsc_pool[16:32, :].bitcast(I32).rearrange("f (u e) -> f u e", u=POOL_PAGES),
             v_scales.rearrange("u f e -> f u e").bitcast(I32),
         )
-        nc.scalar.dma_start(vs_head[:], vs[:, 0:8])
-        nc.scalar.dma_start(planes[0][0:32, q_cols].bitcast(I32), q_scales[0].rearrange("o f q -> (o f) q").bitcast(I32))
+        nc.scalar.dma_start(vs_head[:, 0:8], vs[:, 0:8])
         nc.scalar.dma_start(vs_pool[P - 1 : P, :], vs[0:1, :])
-        nc.sync.dma_start(vcols[:], voffs)
         nc.sync.dma_start(ks_pool[0:32, :].bitcast(I32), k_scales.rearrange("o f t -> (o f) t").bitcast(I32))
+        nc.sync.dma_start(vcols[:], voffs)
         nc.sync.dma_start(slots[:], offs)
+        nc.sync.dma_start(planes[0][0:32, q_cols].bitcast(I32), q_scales[0].rearrange("o f q -> (o f) q").bitcast(I32))
         nc.sync.dma_start(k_pool[:].bitcast(I32), k_words[0].rearrange("p t b -> p (t b)").bitcast(I32))
         nc.sync.dma_start(q_codes[:].bitcast(I32), q_words[0].rearrange("o p q r -> p o (q r)").bitcast(I32))
         nc.sync.dma_start(og_sb[:], og[0])
@@ -77,10 +77,10 @@ def tile_attend_pkv4q_sigm_gate_kernel(
 
         nc.vector.memset(ks_pool[32:64, :].bitcast(I32), 0)
         nc.vector.memset(ks_pool[64:P, :].bitcast(I32), 0)
-        nc.vector.memset(vs_pool[0 : P - 1, 0:SPLIT], 0.0)
 
         nc.vector.memset(planes[0][32:64, q_cols].bitcast(I32), 0)
         nc.vector.memset(planes[0][64:P, q_cols].bitcast(I32), 0)
+        nc.vector.memset(planes[1][:].bitcast(I32), 0)
         nc.scalar.copy(vs_pool[0 : P - 1, SPLIT:T], vs_head[0 : P - 1, 0:1].to_broadcast([P - 1, T - SPLIT]))
 
         vsc_got = own([P, PAGES * DV], U8, "vsc_got")
@@ -88,7 +88,7 @@ def tile_attend_pkv4q_sigm_gate_kernel(
         ks_got = own([P, N], U8, "ks_got")
         nc.vector.tensor_copy(ks_got[:], ks_pool[:].indirect(slots[:]))
         nc.vector.tensor_copy(planes[0][:, N + NQ :].bitcast(I32), vsc_got[:].bitcast(I32))
-        nc.vector.memset(planes[1][:].bitcast(I32), 0)
+        nc.vector.memset(vs_pool[0 : P - 1, 0:SPLIT], 0.0)
         nc.vector.tensor_copy(
             planes[0][:, 0:N].rearrange("p (c t m) -> p c t m", c=PAGES, t=4),
             ks_got[:].rearrange("p (c m t) -> p c t m", c=PAGES, t=4),
@@ -109,23 +109,35 @@ def tile_attend_pkv4q_sigm_gate_kernel(
         def page_slots(c):
             return slots[:, c * 32 : (c + 1) * 32]
 
-        def gather_vs(c):
-            vs_got = own([P, PAGE], F32, f"vs_got{c}")
-            nc.vector.tensor_copy(vs_got[:], vs_pool[:].indirect(page_slots(c)))
-            nc.scalar.dma_start(vs_col[c][:], vs_got[P - 1 : P, :].rearrange("p (m t) -> p m t", t=4))
-
-        k_got = [reusing([P, PAGE], U32, f"k_got{c}", 4 * T * (1 - c)) for c in range(PAGES)]
+        k_got = [reusing([P, PAGE], U32, f"k_got{c}", 4 * PAGE * c) for c in range(PAGES)]
         scores = [psum.tile([P, 2, NQ], F32, name=f"scores{b}", tag=f"bank{b}") for b in range(2 * PAGES)]
-        gather_vs(0)
+        vs_got = own([P, N], F32, "vs_got")
+        nc.vector.tensor_copy(vs_got[:], vs_pool[:].indirect(slots[:]))
+        for c in range(PAGES):
+            row = vs_got[P - 1 : P, c * PAGE : (c + 1) * PAGE]
+            nc.scalar.dma_start(vs_col[c][:], row.rearrange("p (m t) -> p m t", t=4))
         for c in range(PAGES):
             nc.vector.tensor_copy(k_got[c][:], k_pool[:].indirect(page_slots(c)))
-            if c == 0:
-                gather_vs(1)
+        warm = psum.tile([NQ, PAGE], F32, name="warm")
+        nc.tensor.matmul_mx(
+            out=warm[:],
+            lhsT=q_codes[:, 1, :].bitcast(FP8X4),
+            lhsT_scale=planes[1][:, q_cols],
+            rhs=k_got[0][:, 0 : PAGE // 2].bitcast(FP4X4),
+            rhs_scale=planes[1][:, 0:PAGE],
+            start=True,
+            stop=True,
+        )
+        for c in range(PAGES):
             src = k_got[c][:].bitcast(U16).rearrange("p (m t o) -> p o m t", t=4, o=PASSES)
             for a in range(2):
                 k_codes = own([P, PASSES, PAGE], U8, f"k_codes{c}{a}")
                 dst = k_codes[:].bitcast(U16).rearrange("p o (t m) -> p o m t", t=2)
-                nc.vector.tensor_copy(dst, src[:, :, :, 2 * a : 2 * a + 2])
+                if c == 0 and a == 0:
+                    for o in reversed(range(PASSES)):
+                        nc.vector.tensor_copy(dst[:, o], src[:, o, :, 0:2])
+                else:
+                    nc.vector.tensor_copy(dst, src[:, :, :, 2 * a : 2 * a + 2])
                 for t in range(2 * a, 2 * a + 2):
                     for o in reversed(range(PASSES)):
                         nc.tensor.matmul_mx(
@@ -138,7 +150,7 @@ def tile_attend_pkv4q_sigm_gate_kernel(
                             stop=(o == 0),
                         )
 
-        v_got = own([P, PAGES * DV], U32, "v_got", "k_codes01")
+        v_got = own([P, PAGES * DV], U32, "v_got", "k_codes00")
         nc.vector.tensor_copy(v_got[:], v_pool[:].indirect(vcols[:]))
 
         acc = psum.tile([NQ, DV], F32, name="acc")

@@ -9,7 +9,7 @@ PAGES = N // PAGE
 PASSES = D // 512
 POOL_PAGES = T // PAGE
 HALF = NQ // 2
-SPLIT = 512
+SPLIT = 1280
 
 FLOPS = 2 * NQ * N * (D + DV)
 BYTES = P * T * 4 + 32 * T + POOL_PAGES * (P * DV * 4 + 16 * DV) + PASSES * (P * NQ * 4 + 16 * NQ) + T * 4 + 2 * NQ * DV * 4 + P * (N + PAGES * DV) // 8
@@ -50,60 +50,52 @@ def tile_attend_pkv4q_sigm_gate_kernel(
         og_sb = own([P, DV], F32, "og_sb")
         k_pool = own([P, T], U32, "k_pool")
         q_codes = own([P, PASSES, NQ], U32, "q_codes")
-        planes = [own([P, N + NQ + PAGES * DV], U8, "plane0"), own([P, N + NQ + PAGES * DV], U8, "plane1")]
+        planes = [own([P, N + NQ], U8, f"plane{o}") for o in range(PASSES)]
         q_cols = slice(N, N + NQ)
         vsc_pool = own([P, POOL_PAGES * DV], U8, "vsc_pool")
-        for rows in (slice(0, 16), slice(32, 64), slice(64, P)):
-            nc.vector.memset(vsc_pool[rows, :].bitcast(I32), 0)
+        v_pool = own([P, POOL_PAGES * DV], U32, "v_pool")
 
-        nc.scalar.dma_start(
-            vsc_pool[16:32, :].bitcast(I32).rearrange("f (u e) -> f u e", u=POOL_PAGES),
-            v_scales.rearrange("u f e -> f u e").bitcast(I32),
-        )
         nc.scalar.dma_start(vs_head[:, 0:8], vs[:, 0:8])
+        nc.scalar.dma_start(og_sb[:], og[0])
         nc.scalar.dma_start(vs_pool[P - 1 : P, :], vs[0:1, :])
         nc.sync.dma_start(ks_pool[0:32, :].bitcast(I32), k_scales.rearrange("o f t -> (o f) t").bitcast(I32))
-        nc.sync.dma_start(vcols[:], voffs)
         nc.sync.dma_start(slots[:], offs)
         nc.sync.dma_start(planes[0][0:32, q_cols].bitcast(I32), q_scales[0].rearrange("o f q -> (o f) q").bitcast(I32))
-        nc.sync.dma_start(k_pool[:].bitcast(I32), k_words[0].rearrange("p t b -> p (t b)").bitcast(I32))
         nc.sync.dma_start(q_codes[:].bitcast(I32), q_words[0].rearrange("o p q r -> p o (q r)").bitcast(I32))
-        nc.sync.dma_start(og_sb[:], og[0])
-        v_pool = own([P, POOL_PAGES * DV], U32, "v_pool")
-        nc.sync.dma_start(
-            v_pool[:].bitcast(I32).rearrange("p (u e) -> p u e", u=POOL_PAGES),
-            v_words.rearrange("u p e r -> p u (e r)").bitcast(I32),
-        )
+        nc.sync.dma_start(k_pool[:].bitcast(I32), k_words[0].rearrange("p t b -> p (t b)").bitcast(I32))
+        nc.sync.dma_start(vcols[:], voffs)
 
         nc.vector.memset(ks_pool[32:64, :].bitcast(I32), 0)
         nc.vector.memset(ks_pool[64:P, :].bitcast(I32), 0)
-
+        nc.vector.memset(vs_pool[0 : P - 1, 0:SPLIT], 0.0)
         nc.vector.memset(planes[0][32:64, q_cols].bitcast(I32), 0)
         nc.vector.memset(planes[0][64:P, q_cols].bitcast(I32), 0)
         nc.vector.memset(planes[1][:].bitcast(I32), 0)
         nc.scalar.copy(vs_pool[0 : P - 1, SPLIT:T], vs_head[0 : P - 1, 0:1].to_broadcast([P - 1, T - SPLIT]))
 
-        vsc_got = own([P, PAGES * DV], U8, "vsc_got")
-        nc.vector.tensor_copy(vsc_got[:], vsc_pool[:].indirect(vcols[:]))
         ks_got = own([P, N], U8, "ks_got")
         nc.vector.tensor_copy(ks_got[:], ks_pool[:].indirect(slots[:]))
-        nc.vector.tensor_copy(planes[0][:, N + NQ :].bitcast(I32), vsc_got[:].bitcast(I32))
-        nc.vector.memset(vs_pool[0 : P - 1, 0:SPLIT], 0.0)
+        nc.vector.memset(vsc_pool[:].bitcast(I32), 0)
         nc.vector.tensor_copy(
             planes[0][:, 0:N].rearrange("p (c t m) -> p c t m", c=PAGES, t=4),
             ks_got[:].rearrange("p (c m t) -> p c t m", c=PAGES, t=4),
         )
-        for quad in range(1, 4):
-            nc.scalar.dma_start(
-                planes[0][32 * quad : 32 * quad + 4, 0 : N + NQ].bitcast(I32),
-                planes[0][4 * quad : 4 * quad + 4, 0 : N + NQ].bitcast(I32),
-            )
         for r in range(4):
             nc.scalar.dma_start(planes[1][r:P:32, :].bitcast(I32), planes[0][16 + r : 32 : 4, :].bitcast(I32))
+        for quad in range(1, 4):
+            nc.scalar.dma_start(
+                planes[0][32 * quad : 32 * quad + 4, :].bitcast(I32), planes[0][4 * quad : 4 * quad + 4, :].bitcast(I32)
+            )
 
-        gate = own([NQ, DV], F32, "gate")
-        nc.scalar.activation(gate[:], og_sb[:], SIGMOID)
-
+        nc.scalar.dma_start(
+            v_pool[:].bitcast(I32).rearrange("p (u e) -> p u e", u=POOL_PAGES),
+            v_words.rearrange("u p e r -> p u (e r)").bitcast(I32),
+        )
+        for quad in range(4):
+            nc.scalar.dma_start(
+                vsc_pool[32 * quad : 32 * quad + 4, :].bitcast(I32).rearrange("f (u e) -> f u e", u=POOL_PAGES),
+                v_scales[:, 4 * quad : 4 * quad + 4, :].rearrange("u f e -> f u e").bitcast(I32),
+            )
         vs_col = [own([P, 4], F32, f"vs_col{c}") for c in range(PAGES)]
 
         def page_slots(c):
@@ -116,6 +108,8 @@ def tile_attend_pkv4q_sigm_gate_kernel(
         for c in range(PAGES):
             row = vs_got[P - 1 : P, c * PAGE : (c + 1) * PAGE]
             nc.scalar.dma_start(vs_col[c][:], row.rearrange("p (m t) -> p m t", t=4))
+        gate = own([NQ, DV], F32, "gate")
+        nc.scalar.activation(gate[:], og_sb[:], SIGMOID)
         for c in range(PAGES):
             nc.vector.tensor_copy(k_got[c][:], k_pool[:].indirect(page_slots(c)))
         warm = psum.tile([NQ, PAGE], F32, name="warm")
@@ -134,24 +128,27 @@ def tile_attend_pkv4q_sigm_gate_kernel(
                 k_codes = own([P, PASSES, PAGE], U8, f"k_codes{c}{a}")
                 dst = k_codes[:].bitcast(U16).rearrange("p o (t m) -> p o m t", t=2)
                 if c == 0 and a == 0:
-                    for o in reversed(range(PASSES)):
+                    for o in range(PASSES):
                         nc.vector.tensor_copy(dst[:, o], src[:, o, :, 0:2])
                 else:
                     nc.vector.tensor_copy(dst, src[:, :, :, 2 * a : 2 * a + 2])
                 for t in range(2 * a, 2 * a + 2):
-                    for o in reversed(range(PASSES)):
+                    for o in range(PASSES):
                         nc.tensor.matmul_mx(
                             out=scores[2 * c + a][:, t % 2, :],
                             lhsT=k_codes[:, o, 256 * (t % 2) : 256 * (t % 2 + 1)].bitcast(FP4X4),
                             lhsT_scale=planes[o][:, c * PAGE + P * t : c * PAGE + P * (t + 1)],
                             rhs=q_codes[:, o, :].bitcast(FP8X4),
                             rhs_scale=planes[o][:, q_cols],
-                            start=(o == PASSES - 1),
-                            stop=(o == 0),
+                            start=(o == 0),
+                            stop=(o == PASSES - 1),
                         )
 
         v_got = own([P, PAGES * DV], U32, "v_got", "k_codes00")
         nc.vector.tensor_copy(v_got[:], v_pool[:].indirect(vcols[:]))
+
+        v_plane = own([P, PAGES * DV], U8, "v_plane")
+        nc.vector.tensor_copy(v_plane[:], vsc_pool[:].indirect(vcols[:]))
 
         acc = psum.tile([NQ, DV], F32, name="acc")
         halves = [slice(h * HALF, (h + 1) * HALF) for h in range(2)]
@@ -183,7 +180,7 @@ def tile_attend_pkv4q_sigm_gate_kernel(
                 lhsT=w_codes[:].bitcast(FP8X4),
                 lhsT_scale=w_plane[:],
                 rhs=v_got[:, c * DV : (c + 1) * DV].bitcast(FP8X4),
-                rhs_scale=planes[1][:, N + NQ + c * DV : N + NQ + (c + 1) * DV],
+                rhs_scale=v_plane[:, c * DV : (c + 1) * DV],
                 start=(c == 0),
                 stop=(c == PAGES - 1),
             )

@@ -55,15 +55,18 @@ def tile_attend_pkv4q_sigm_gate_kernel(
         vsc_pool = own([P, POOL_PAGES * DV], U8, "vsc_pool")
         v_pool = own([P, POOL_PAGES * DV], U32, "v_pool")
 
-        nc.scalar.dma_start(vs_head[:, 0:8], vs[:, 0:8])
-        nc.scalar.dma_start(og_sb[:], og[0])
-        nc.scalar.dma_start(vs_pool[P - 1 : P, :], vs[0:1, :])
         nc.sync.dma_start(ks_pool[0:32, :].bitcast(I32), k_scales.rearrange("o f t -> (o f) t").bitcast(I32))
         nc.sync.dma_start(slots[:], offs)
-        nc.sync.dma_start(planes[0][0:32, q_cols].bitcast(I32), q_scales[0].rearrange("o f q -> (o f) q").bitcast(I32))
-        nc.sync.dma_start(q_codes[:].bitcast(I32), q_words[0].rearrange("o p q r -> p o (q r)").bitcast(I32))
-        nc.sync.dma_start(k_pool[:].bitcast(I32), k_words[0].rearrange("p t b -> p (t b)").bitcast(I32))
-        nc.sync.dma_start(vcols[:], voffs)
+        nc.sync.dma_start(vs_pool[P - 1 : P, :], vs[0:1, :])
+        nc.scalar.dma_start(og_sb[:], og[0])
+        nc.scalar.dma_start(vs_head[:, 0:8], vs[:, 0:8])
+        nc.scalar.dma_start(planes[0][0:32, q_cols].bitcast(I32), q_scales[0].rearrange("o f q -> (o f) q").bitcast(I32))
+        nc.scalar.dma_start(q_codes[:].bitcast(I32), q_words[0].rearrange("o p q r -> p o (q r)").bitcast(I32))
+        nc.scalar.dma_start(
+            k_pool[:].bitcast(I32), k_words[0].rearrange("p t b -> p (t b)").bitcast(I32), max_dma_last_dim=2048
+        )
+        gate = own([NQ, DV], F32, "gate")
+        nc.scalar.activation(gate[:], og_sb[:], SIGMOID)
 
         nc.vector.memset(ks_pool[32:64, :].bitcast(I32), 0)
         nc.vector.memset(ks_pool[64:P, :].bitcast(I32), 0)
@@ -81,18 +84,19 @@ def tile_attend_pkv4q_sigm_gate_kernel(
             ks_got[:].rearrange("p (c m t) -> p c t m", c=PAGES, t=4),
         )
         for r in range(4):
-            nc.scalar.dma_start(planes[1][r:P:32, :].bitcast(I32), planes[0][16 + r : 32 : 4, :].bitcast(I32))
+            nc.sync.dma_start(planes[1][r:P:32, :].bitcast(I32), planes[0][16 + r : 32 : 4, :].bitcast(I32))
         for quad in range(1, 4):
-            nc.scalar.dma_start(
+            nc.sync.dma_start(
                 planes[0][32 * quad : 32 * quad + 4, :].bitcast(I32), planes[0][4 * quad : 4 * quad + 4, :].bitcast(I32)
             )
 
-        nc.scalar.dma_start(
+        nc.sync.dma_start(vcols[:], voffs)
+        nc.sync.dma_start(
             v_pool[:].bitcast(I32).rearrange("p (u e) -> p u e", u=POOL_PAGES),
             v_words.rearrange("u p e r -> p u (e r)").bitcast(I32),
         )
         for quad in range(4):
-            nc.scalar.dma_start(
+            nc.sync.dma_start(
                 vsc_pool[32 * quad : 32 * quad + 4, :].bitcast(I32).rearrange("f (u e) -> f u e", u=POOL_PAGES),
                 v_scales[:, 4 * quad : 4 * quad + 4, :].rearrange("u f e -> f u e").bitcast(I32),
             )
@@ -107,9 +111,7 @@ def tile_attend_pkv4q_sigm_gate_kernel(
         nc.vector.tensor_copy(vs_got[:], vs_pool[:].indirect(slots[:]))
         for c in range(PAGES):
             row = vs_got[P - 1 : P, c * PAGE : (c + 1) * PAGE]
-            nc.scalar.dma_start(vs_col[c][:], row.rearrange("p (m t) -> p m t", t=4))
-        gate = own([NQ, DV], F32, "gate")
-        nc.scalar.activation(gate[:], og_sb[:], SIGMOID)
+            nc.sync.dma_start(vs_col[c][:], row.rearrange("p (m t) -> p m t", t=4))
         for c in range(PAGES):
             nc.vector.tensor_copy(k_got[c][:], k_pool[:].indirect(page_slots(c)))
         warm = psum.tile([NQ, PAGE], F32, name="warm")

@@ -9,7 +9,7 @@ PAGES = N // PAGE
 PASSES = D // 512
 POOL_PAGES = T // PAGE
 HALF = NQ // 2
-SPLIT = 1280
+SPLIT = 896
 
 FLOPS = 2 * NQ * N * (D + DV)
 BYTES = P * T * 4 + 32 * T + POOL_PAGES * (P * DV * 4 + 16 * DV) + PASSES * (P * NQ * 4 + 16 * NQ) + T * 4 + 2 * NQ * DV * 4 + P * (N + PAGES * DV) // 8
@@ -50,56 +50,56 @@ def tile_attend_pkv4q_sigm_gate_kernel(
         og_sb = own([P, DV], F32, "og_sb")
         k_pool = own([P, T], U32, "k_pool")
         q_codes = own([P, PASSES, NQ], U32, "q_codes")
-        planes = [own([P, N + NQ], U8, f"plane{o}") for o in range(PASSES)]
+        staged = own([P, N + NQ], U8, "staged")
+        both = own([P, PASSES, N + NQ], U8, "both")
+        v_plane = own([P, PAGES * DV], U8, "v_plane")
+        planes = [both[:, o, :] for o in range(PASSES)]
         q_cols = slice(N, N + NQ)
         vsc_pool = own([P, POOL_PAGES * DV], U8, "vsc_pool")
         v_pool = own([P, POOL_PAGES * DV], U32, "v_pool")
 
-        nc.sync.dma_start(ks_pool[0:32, :].bitcast(I32), k_scales.rearrange("o f t -> (o f) t").bitcast(I32))
+        nc.sync.dma_start(vcols[:], voffs)
+        nc.sync.dma_start(ks_pool[0:32, :].bitcast(I32), k_scales.rearrange("o f t -> f o t").bitcast(I32))
         nc.sync.dma_start(slots[:], offs)
-        nc.sync.dma_start(vs_pool[P - 1 : P, :], vs[0:1, :])
-        nc.scalar.dma_start(og_sb[:], og[0])
-        nc.scalar.dma_start(vs_head[:, 0:8], vs[:, 0:8])
-        nc.scalar.dma_start(planes[0][0:32, q_cols].bitcast(I32), q_scales[0].rearrange("o f q -> (o f) q").bitcast(I32))
-        nc.scalar.dma_start(q_codes[:].bitcast(I32), q_words[0].rearrange("o p q r -> p o (q r)").bitcast(I32))
+        nc.sync.dma_start(k_pool[:].bitcast(I32), k_words[0].rearrange("p t b -> p (t b)").bitcast(I32))
+        nc.sync.dma_start(og_sb[:], og[0])
+        nc.sync.dma_start(q_codes[:].bitcast(I32), q_words[0].rearrange("o p q r -> p o (q r)").bitcast(I32))
         nc.scalar.dma_start(
-            k_pool[:].bitcast(I32), k_words[0].rearrange("p t b -> p (t b)").bitcast(I32), max_dma_last_dim=2048
+            vsc_pool[P - 16 : P, :].bitcast(I32).rearrange("f (u e) -> f u e", u=POOL_PAGES),
+            v_scales.rearrange("u f e -> f u e").bitcast(I32),
         )
-        gate = own([NQ, DV], F32, "gate")
-        nc.scalar.activation(gate[:], og_sb[:], SIGMOID)
+        nc.scalar.dma_start(vs_head[:, 0:8], vs[:, 0:8])
+        nc.scalar.dma_start(staged[0:32, q_cols].bitcast(I32), q_scales[0].rearrange("o f q -> f o q").bitcast(I32))
+        nc.scalar.dma_start(vs_pool[P - 1 : P, :], vs[0:1, :])
 
+        nc.vector.memset(vsc_pool[0 : P - 16, :].bitcast(I32), 0)
         nc.vector.memset(ks_pool[32:64, :].bitcast(I32), 0)
         nc.vector.memset(ks_pool[64:P, :].bitcast(I32), 0)
         nc.vector.memset(vs_pool[0 : P - 1, 0:SPLIT], 0.0)
-        nc.vector.memset(planes[0][32:64, q_cols].bitcast(I32), 0)
-        nc.vector.memset(planes[0][64:P, q_cols].bitcast(I32), 0)
-        nc.vector.memset(planes[1][:].bitcast(I32), 0)
+        nc.vector.memset(v_plane[:].bitcast(I32), 0)
         nc.scalar.copy(vs_pool[0 : P - 1, SPLIT:T], vs_head[0 : P - 1, 0:1].to_broadcast([P - 1, T - SPLIT]))
+        gate = own([NQ, DV], F32, "gate")
+        nc.scalar.activation(gate[:], og_sb[:], SIGMOID)
 
+        vsc_got = own([P, PAGES * DV], U8, "vsc_got")
+        nc.vector.tensor_copy(vsc_got[:], vsc_pool[:].indirect(vcols[:]))
         ks_got = own([P, N], U8, "ks_got")
         nc.vector.tensor_copy(ks_got[:], ks_pool[:].indirect(slots[:]))
-        nc.vector.memset(vsc_pool[:].bitcast(I32), 0)
+        nc.vector.memset(both[:].rearrange("p o c -> p (o c)").bitcast(I32), 0)
         nc.vector.tensor_copy(
-            planes[0][:, 0:N].rearrange("p (c t m) -> p c t m", c=PAGES, t=4),
+            staged[:, 0:N].rearrange("p (c t m) -> p c t m", c=PAGES, t=4),
             ks_got[:].rearrange("p (c m t) -> p c t m", c=PAGES, t=4),
         )
-        for r in range(4):
-            nc.sync.dma_start(planes[1][r:P:32, :].bitcast(I32), planes[0][16 + r : 32 : 4, :].bitcast(I32))
-        for quad in range(1, 4):
-            nc.sync.dma_start(
-                planes[0][32 * quad : 32 * quad + 4, :].bitcast(I32), planes[0][4 * quad : 4 * quad + 4, :].bitcast(I32)
-            )
+        for quad in range(4):
+            nc.sync.dma_start(both[32 * quad : 32 * quad + 4].bitcast(I32), staged[8 * quad : 8 * quad + 8, :].bitcast(I32))
 
-        nc.sync.dma_start(vcols[:], voffs)
         nc.sync.dma_start(
             v_pool[:].bitcast(I32).rearrange("p (u e) -> p u e", u=POOL_PAGES),
             v_words.rearrange("u p e r -> p u (e r)").bitcast(I32),
         )
         for quad in range(4):
-            nc.sync.dma_start(
-                vsc_pool[32 * quad : 32 * quad + 4, :].bitcast(I32).rearrange("f (u e) -> f u e", u=POOL_PAGES),
-                v_scales[:, 4 * quad : 4 * quad + 4, :].rearrange("u f e -> f u e").bitcast(I32),
-            )
+            rows = vsc_got[P - 16 + 4 * quad : P - 12 + 4 * quad, :]
+            nc.sync.dma_start(v_plane[32 * quad : 32 * quad + 4, :].bitcast(I32), rows.bitcast(I32))
         vs_col = [own([P, 4], F32, f"vs_col{c}") for c in range(PAGES)]
 
         def page_slots(c):
@@ -149,8 +149,6 @@ def tile_attend_pkv4q_sigm_gate_kernel(
         v_got = own([P, PAGES * DV], U32, "v_got", "k_codes00")
         nc.vector.tensor_copy(v_got[:], v_pool[:].indirect(vcols[:]))
 
-        v_plane = own([P, PAGES * DV], U8, "v_plane")
-        nc.vector.tensor_copy(v_plane[:], vsc_pool[:].indirect(vcols[:]))
 
         acc = psum.tile([NQ, DV], F32, name="acc")
         halves = [slice(h * HALF, (h + 1) * HALF) for h in range(2)]

@@ -9,7 +9,7 @@ PAGES = N // PAGE
 PASSES = D // 512
 POOL_PAGES = T // PAGE
 HALF = NQ // 2
-SPLIT = 896
+SPLIT = 1280
 
 FLOPS = 2 * NQ * N * (D + DV)
 BYTES = P * T * 4 + 32 * T + POOL_PAGES * (P * DV * 4 + 16 * DV) + PASSES * (P * NQ * 4 + 16 * NQ) + T * 4 + 2 * NQ * DV * 4 + P * (N + PAGES * DV) // 8
@@ -58,34 +58,34 @@ def tile_attend_pkv4q_sigm_gate_kernel(
         vsc_pool = own([P, POOL_PAGES * DV], U8, "vsc_pool")
         v_pool = own([P, POOL_PAGES * DV], U32, "v_pool")
 
-        nc.sync.dma_start(vcols[:], voffs)
         nc.sync.dma_start(ks_pool[0:32, :].bitcast(I32), k_scales.rearrange("o f t -> f o t").bitcast(I32))
         nc.sync.dma_start(slots[:], offs)
+        nc.sync.dma_start(vcols[:], voffs)
         nc.sync.dma_start(k_pool[:].bitcast(I32), k_words[0].rearrange("p t b -> p (t b)").bitcast(I32))
         nc.sync.dma_start(og_sb[:], og[0])
         nc.sync.dma_start(q_codes[:].bitcast(I32), q_words[0].rearrange("o p q r -> p o (q r)").bitcast(I32))
+        nc.scalar.dma_start(vs_head[:, 0:8], vs[:, 0:8])
+        nc.scalar.dma_start(staged[0:32, q_cols].bitcast(I32), q_scales[0].rearrange("o f q -> f o q").bitcast(I32))
         nc.scalar.dma_start(
             vsc_pool[P - 16 : P, :].bitcast(I32).rearrange("f (u e) -> f u e", u=POOL_PAGES),
             v_scales.rearrange("u f e -> f u e").bitcast(I32),
         )
-        nc.scalar.dma_start(vs_head[:, 0:8], vs[:, 0:8])
-        nc.scalar.dma_start(staged[0:32, q_cols].bitcast(I32), q_scales[0].rearrange("o f q -> f o q").bitcast(I32))
         nc.scalar.dma_start(vs_pool[P - 1 : P, :], vs[0:1, :])
 
         nc.vector.memset(vsc_pool[0 : P - 16, :].bitcast(I32), 0)
         nc.vector.memset(ks_pool[32:64, :].bitcast(I32), 0)
         nc.vector.memset(ks_pool[64:P, :].bitcast(I32), 0)
         nc.vector.memset(vs_pool[0 : P - 1, 0:SPLIT], 0.0)
+        nc.vector.memset(both[:].rearrange("p o c -> p (o c)").bitcast(I32), 0)
         nc.vector.memset(v_plane[:].bitcast(I32), 0)
         nc.scalar.copy(vs_pool[0 : P - 1, SPLIT:T], vs_head[0 : P - 1, 0:1].to_broadcast([P - 1, T - SPLIT]))
         gate = own([NQ, DV], F32, "gate")
         nc.scalar.activation(gate[:], og_sb[:], SIGMOID)
 
-        vsc_got = own([P, PAGES * DV], U8, "vsc_got")
-        nc.vector.tensor_copy(vsc_got[:], vsc_pool[:].indirect(vcols[:]))
         ks_got = own([P, N], U8, "ks_got")
         nc.vector.tensor_copy(ks_got[:], ks_pool[:].indirect(slots[:]))
-        nc.vector.memset(both[:].rearrange("p o c -> p (o c)").bitcast(I32), 0)
+        vsc_got = own([P, PAGES * DV], U8, "vsc_got")
+        nc.vector.tensor_copy(vsc_got[:], vsc_pool[:].indirect(vcols[:]))
         nc.vector.tensor_copy(
             staged[:, 0:N].rearrange("p (c t m) -> p c t m", c=PAGES, t=4),
             ks_got[:].rearrange("p (c m t) -> p c t m", c=PAGES, t=4),

@@ -114,16 +114,6 @@ def tile_attend_pkv4q_sigm_gate_kernel(
             nc.sync.dma_start(vs_col[c][:], row.rearrange("p (m t) -> p m t", t=4))
         for c in range(PAGES):
             nc.vector.tensor_copy(k_got[c][:], k_pool[:].indirect(page_slots(c)))
-        warm = psum.tile([NQ, PAGE], F32, name="warm")
-        nc.tensor.matmul_mx(
-            out=warm[:],
-            lhsT=q_codes[:, 1, :].bitcast(FP8X4),
-            lhsT_scale=planes[1][:, q_cols],
-            rhs=k_got[0][:, 0 : PAGE // 2].bitcast(FP4X4),
-            rhs_scale=planes[1][:, 0:PAGE],
-            start=True,
-            stop=True,
-        )
         for c in range(PAGES):
             src = k_got[c][:].bitcast(U16).rearrange("p (m t o) -> p o m t", t=4, o=PASSES)
             for a in range(2):

@@ -24,6 +24,7 @@ FP8X4 = mybir.dt.float8_e4m3fn_x4
 FP4X4 = mybir.dt.float4_e2m1fn_x4
 MULT = mybir.AluOpType.mult
 SIGMOID = mybir.ActivationFunctionType.Sigmoid
+COPY = mybir.ActivationFunctionType.Copy
 
 
 def tile_attend_pkv4q_sigm_gate_kernel(
@@ -33,20 +34,16 @@ def tile_attend_pkv4q_sigm_gate_kernel(
     with ExitStack() as ctx:
         lists = ctx.enter_context(tc.tile_pool(name="lists", bufs=1))
         held = ctx.enter_context(tc.tile_pool(name="held", bufs=1))
-        reused = ctx.enter_context(tc.tile_pool(name="reused", bufs=1))
         psum = ctx.enter_context(tc.psum_pool(name="psum", bufs=1))
 
         def own(shape, dtype, name, tag=None):
             return held.tile(shape, dtype, name=name, tag=tag or name, align_bytes=64)
 
-        def reusing(shape, dtype, name, offset):
-            return reused.tile(shape, dtype, name=name, offset=offset, align_bytes=64)
-
         slots = lists.tile([P, N // 16], U16, name="slots")
         vcols = lists.tile([P, PAGES * DV // 16], U16, name="vcols")
         ks_pool = own([P, T], U8, "ks_pool")
         vs_pool = own([P, T], F32, "vs_pool")
-        vs_head = reusing([P, 32], F32, "vs_head", 4 * PAGE - 64)
+        vs_head = own([P, 8], F32, "vs_head")
         og_sb = own([P, DV], F32, "og_sb")
         k_pool = own([P, T], U32, "k_pool")
         q_codes = own([P, PASSES, NQ], U32, "q_codes")
@@ -79,8 +76,6 @@ def tile_attend_pkv4q_sigm_gate_kernel(
         nc.vector.memset(both[:].rearrange("p o c -> p (o c)").bitcast(I32), 0)
         nc.vector.memset(v_plane[:].bitcast(I32), 0)
         nc.scalar.copy(vs_pool[0 : P - 1, SPLIT:T], vs_head[0 : P - 1, 0:1].to_broadcast([P - 1, T - SPLIT]))
-        gate = own([NQ, DV], F32, "gate")
-        nc.scalar.activation(gate[:], og_sb[:], SIGMOID)
 
         ks_got = own([P, N], U8, "ks_got")
         nc.vector.tensor_copy(ks_got[:], ks_pool[:].indirect(slots[:]))
@@ -102,33 +97,32 @@ def tile_attend_pkv4q_sigm_gate_kernel(
             nc.sync.dma_start(v_plane[32 * quad : 32 * quad + 4, :].bitcast(I32), rows.bitcast(I32))
         vs_col = [own([P, 4], F32, f"vs_col{c}") for c in range(PAGES)]
 
-        def page_slots(c):
-            return slots[:, c * 32 : (c + 1) * 32]
-
-        k_got = [reusing([P, PAGE], U32, f"k_got{c}", 4 * PAGE * c) for c in range(PAGES)]
         scores = [psum.tile([P, 2, NQ], F32, name=f"scores{b}", tag=f"bank{b}") for b in range(2 * PAGES)]
         vs_got = own([P, N], F32, "vs_got")
-        nc.vector.tensor_copy(vs_got[:], vs_pool[:].indirect(slots[:]))
         for c in range(PAGES):
+            nc.scalar.activation(vs_got[:, c * PAGE : (c + 1) * PAGE], vs_pool[:].indirect(slots[:, 32 * c : 32 * (c + 1)]), COPY)
             row = vs_got[P - 1 : P, c * PAGE : (c + 1) * PAGE]
-            nc.sync.dma_start(vs_col[c][:], row.rearrange("p (m t) -> p m t", t=4))
+            nc.scalar.dma_start(vs_col[c][:], row.rearrange("p (m t) -> p m t", t=4))
+        gate = own([NQ, DV], F32, "gate")
+        nc.scalar.activation(gate[:], og_sb[:], SIGMOID)
         for c in range(PAGES):
-            nc.vector.tensor_copy(k_got[c][:], k_pool[:].indirect(page_slots(c)))
-        for c in range(PAGES):
-            src = k_got[c][:].bitcast(U16).rearrange("p (m t o) -> p o m t", t=4, o=PASSES)
+            k_got = []
+            for h in range(2):
+                half = held.tile([P, PAGE // 2], U32, name=f"k_got{c}{h}", tag="k_got", bufs=2, align_bytes=64)
+                nc.vector.tensor_copy(half[:], k_pool[:].indirect(slots[:, 32 * c + 16 * h : 32 * c + 16 * (h + 1)]))
+                k_got.append(half)
+            k_codes = [own([P, PASSES, PAGE], U8, f"k_codes{c}{a}") for a in range(2)]
+            for h in range(2):
+                src = k_got[h][:].bitcast(U16).rearrange("p (m t o) -> p o m t", t=4, o=PASSES)
+                for a in range(2):
+                    dst = k_codes[a][:].bitcast(U16).rearrange("p o (t m) -> p o m t", t=2)
+                    nc.vector.tensor_copy(dst[:, :, 64 * h : 64 * (h + 1), :], src[:, :, :, 2 * a : 2 * a + 2])
             for a in range(2):
-                k_codes = own([P, PASSES, PAGE], U8, f"k_codes{c}{a}")
-                dst = k_codes[:].bitcast(U16).rearrange("p o (t m) -> p o m t", t=2)
-                if c == 0 and a == 0:
-                    for o in range(PASSES):
-                        nc.vector.tensor_copy(dst[:, o], src[:, o, :, 0:2])
-                else:
-                    nc.vector.tensor_copy(dst, src[:, :, :, 2 * a : 2 * a + 2])
                 for t in range(2 * a, 2 * a + 2):
                     for o in range(PASSES):
                         nc.tensor.matmul_mx(
                             out=scores[2 * c + a][:, t % 2, :],
-                            lhsT=k_codes[:, o, 256 * (t % 2) : 256 * (t % 2 + 1)].bitcast(FP4X4),
+                            lhsT=k_codes[a][:, o, 256 * (t % 2) : 256 * (t % 2 + 1)].bitcast(FP4X4),
                             lhsT_scale=planes[o][:, c * PAGE + P * t : c * PAGE + P * (t + 1)],
                             rhs=q_codes[:, o, :].bitcast(FP8X4),
                             rhs_scale=planes[o][:, q_cols],
@@ -136,7 +130,7 @@ def tile_attend_pkv4q_sigm_gate_kernel(
                             stop=(o == PASSES - 1),
                         )
 
-        v_got = own([P, PAGES * DV], U32, "v_got", "k_codes00")
+        v_got = held.tile([P, PAGES * DV], U32, name="v_got", tag="k_got", bufs=2, align_bytes=64)
         nc.vector.tensor_copy(v_got[:], v_pool[:].indirect(vcols[:]))
 
 

@@ -85,7 +85,7 @@ def tile_attend_pkv4q_sigm_gate_kernel(
             staged[:, 0:N].rearrange("p (c t m) -> p c t m", c=PAGES, t=4),
             ks_got[:].rearrange("p (c m t) -> p c t m", c=PAGES, t=4),
         )
-        for quad in range(4):
+        for quad in (0, 2, 1, 3):
             nc.sync.dma_start(both[32 * quad : 32 * quad + 4].bitcast(I32), staged[8 * quad : 8 * quad + 8, :].bitcast(I32))
 
         nc.sync.dma_start(
@@ -111,24 +111,24 @@ def tile_attend_pkv4q_sigm_gate_kernel(
                 half = held.tile([P, PAGE // 2], U32, name=f"k_got{c}{h}", tag="k_got", bufs=2, align_bytes=64)
                 nc.vector.tensor_copy(half[:], k_pool[:].indirect(slots[:, 32 * c + 16 * h : 32 * c + 16 * (h + 1)]))
                 k_got.append(half)
-            k_codes = [own([P, PASSES, PAGE], U8, f"k_codes{c}{a}") for a in range(2)]
+            k_codes = own([P, PASSES, 2 * PAGE], U8, f"k_codes{c}")
+            dst = k_codes[:].bitcast(U16).rearrange("p o (t m) -> p o m t", t=4)
             for h in range(2):
                 src = k_got[h][:].bitcast(U16).rearrange("p (m t o) -> p o m t", t=4, o=PASSES)
-                for a in range(2):
-                    dst = k_codes[a][:].bitcast(U16).rearrange("p o (t m) -> p o m t", t=2)
-                    nc.vector.tensor_copy(dst[:, :, 64 * h : 64 * (h + 1), :], src[:, :, :, 2 * a : 2 * a + 2])
-            for a in range(2):
-                for t in range(2 * a, 2 * a + 2):
-                    for o in range(PASSES):
-                        nc.tensor.matmul_mx(
-                            out=scores[2 * c + a][:, t % 2, :],
-                            lhsT=k_codes[a][:, o, 256 * (t % 2) : 256 * (t % 2 + 1)].bitcast(FP4X4),
-                            lhsT_scale=planes[o][:, c * PAGE + P * t : c * PAGE + P * (t + 1)],
-                            rhs=q_codes[:, o, :].bitcast(FP8X4),
-                            rhs_scale=planes[o][:, q_cols],
-                            start=(o == 0),
-                            stop=(o == PASSES - 1),
-                        )
+                last = c == PAGES - 1 and h == 1
+                for ts in [slice(t, t + 1) for t in range(4)] if last else [slice(0, 4)]:
+                    nc.vector.tensor_copy(dst[:, :, 64 * h : 64 * (h + 1), ts], src[:, :, :, ts])
+            for t in range(4):
+                for o in range(PASSES):
+                    nc.tensor.matmul_mx(
+                        out=scores[2 * c + t // 2][:, t % 2, :],
+                        lhsT=k_codes[:, o, 256 * t : 256 * (t + 1)].bitcast(FP4X4),
+                        lhsT_scale=planes[o][:, c * PAGE + P * t : c * PAGE + P * (t + 1)],
+                        rhs=q_codes[:, o, :].bitcast(FP8X4),
+                        rhs_scale=planes[o][:, q_cols],
+                        start=(o == 0),
+                        stop=(o == PASSES - 1),
+                    )
 
         v_got = held.tile([P, PAGES * DV], U32, name="v_got", tag="k_got", bufs=2, align_bytes=64)
         nc.vector.tensor_copy(v_got[:], v_pool[:].indirect(vcols[:]))

@@ -59,7 +59,6 @@ def tile_attend_pkv4q_sigm_gate_kernel(
         nc.sync.dma_start(slots[:], offs)
         nc.sync.dma_start(vcols[:], voffs)
         nc.sync.dma_start(k_pool[:].bitcast(I32), k_words[0].rearrange("p t b -> p (t b)").bitcast(I32))
-        nc.sync.dma_start(og_sb[:], og[0])
         nc.sync.dma_start(q_codes[:].bitcast(I32), q_words[0].rearrange("o p q r -> p o (q r)").bitcast(I32))
         nc.scalar.dma_start(vs_head[:, 0:8], vs[:, 0:8])
         nc.scalar.dma_start(staged[0:32, q_cols].bitcast(I32), q_scales[0].rearrange("o f q -> f o q").bitcast(I32))
@@ -87,14 +86,12 @@ def tile_attend_pkv4q_sigm_gate_kernel(
         )
         for quad in (0, 2, 1, 3):
             nc.sync.dma_start(both[32 * quad : 32 * quad + 4].bitcast(I32), staged[8 * quad : 8 * quad + 8, :].bitcast(I32))
+        nc.sync.dma_start(og_sb[:], og[0])
 
         nc.sync.dma_start(
             v_pool[:].bitcast(I32).rearrange("p (u e) -> p u e", u=POOL_PAGES),
             v_words.rearrange("u p e r -> p u (e r)").bitcast(I32),
         )
-        for quad in range(4):
-            rows = vsc_got[P - 16 + 4 * quad : P - 12 + 4 * quad, :]
-            nc.sync.dma_start(v_plane[32 * quad : 32 * quad + 4, :].bitcast(I32), rows.bitcast(I32))
         vs_col = [own([P, 4], F32, f"vs_col{c}") for c in range(PAGES)]
 
         scores = [psum.tile([P, 2, NQ], F32, name=f"scores{b}", tag=f"bank{b}") for b in range(2 * PAGES)]
@@ -102,7 +99,10 @@ def tile_attend_pkv4q_sigm_gate_kernel(
         for c in range(PAGES):
             nc.scalar.activation(vs_got[:, c * PAGE : (c + 1) * PAGE], vs_pool[:].indirect(slots[:, 32 * c : 32 * (c + 1)]), COPY)
             row = vs_got[P - 1 : P, c * PAGE : (c + 1) * PAGE]
-            nc.scalar.dma_start(vs_col[c][:], row.rearrange("p (m t) -> p m t", t=4))
+            nc.sync.dma_start(vs_col[c][:], row.rearrange("p (m t) -> p m t", t=4))
+        for quad in range(4):
+            rows = vsc_got[P - 16 + 4 * quad : P - 12 + 4 * quad, :]
+            nc.sync.dma_start(v_plane[32 * quad : 32 * quad + 4, :].bitcast(I32), rows.bitcast(I32))
         gate = own([NQ, DV], F32, "gate")
         nc.scalar.activation(gate[:], og_sb[:], SIGMOID)
         for c in range(PAGES):

@@ -76,14 +76,16 @@ def tile_attend_pkv4q_sigm_gate_kernel(
         nc.vector.memset(v_plane[:].bitcast(I32), 0)
         nc.scalar.copy(vs_pool[0 : P - 1, SPLIT:T], vs_head[0 : P - 1, 0:1].to_broadcast([P - 1, T - SPLIT]))
 
-        ks_got = own([P, N], U8, "ks_got")
-        nc.vector.tensor_copy(ks_got[:], ks_pool[:].indirect(slots[:]))
-        vsc_got = own([P, PAGES * DV], U8, "vsc_got")
+        ks_got = own([P, PAGES, PAGE], U8, "ks_got")
+        for c in range(PAGES):
+            nc.vector.tensor_copy(ks_got[:, c, :], ks_pool[:].indirect(slots[:, 32 * c : 32 * (c + 1)]))
+        for c in range(PAGES):
+            nc.vector.tensor_copy(
+                staged[:, c * PAGE : (c + 1) * PAGE].rearrange("p (t m) -> p t m", t=4),
+                ks_got[:, c, :].rearrange("p (m t) -> p t m", t=4),
+            )
+        vsc_got = own([P, PAGES * DV], U8, "vsc_got", tag="ks_got")
         nc.vector.tensor_copy(vsc_got[:], vsc_pool[:].indirect(vcols[:]))
-        nc.vector.tensor_copy(
-            staged[:, 0:N].rearrange("p (c t m) -> p c t m", c=PAGES, t=4),
-            ks_got[:].rearrange("p (c m t) -> p c t m", c=PAGES, t=4),
-        )
         for quad in (0, 2, 1, 3):
             nc.sync.dma_start(both[32 * quad : 32 * quad + 4].bitcast(I32), staged[8 * quad : 8 * quad + 8, :].bitcast(I32))
         nc.sync.dma_start(og_sb[:], og[0])

@@ -45,7 +45,7 @@ def tile_attend_pkv4q_sigm_gate_kernel(
         vs_pool = own([P, T], F32, "vs_pool")
         vs_head = own([P, 8], F32, "vs_head")
         og_sb = own([P, DV], F32, "og_sb")
-        k_pool = own([P, T], U32, "k_pool")
+        k_pool = [own([P, T], U32, f"k_pool{h}") for h in range(2)]
         q_codes = own([P, PASSES, NQ], U32, "q_codes")
         staged = own([P, N + NQ], U8, "staged")
         both = own([P, PASSES, N + NQ], U8, "both")
@@ -58,7 +58,11 @@ def tile_attend_pkv4q_sigm_gate_kernel(
         nc.sync.dma_start(ks_pool[0:32, :].bitcast(I32), k_scales.rearrange("o f t -> f o t").bitcast(I32))
         nc.sync.dma_start(slots[:], offs)
         nc.sync.dma_start(vcols[:], voffs)
-        nc.sync.dma_start(k_pool[:].bitcast(I32), k_words[0].rearrange("p t b -> p (t b)").bitcast(I32))
+        for h in range(2):
+            cols = slice(h * PAGE // 2, (h + 1) * PAGE // 2)
+            src = k_words[0].rearrange("p t b -> p (t b)").bitcast(I32).rearrange("p (u j) -> p u j", u=POOL_PAGES)
+            dst = k_pool[h][:].bitcast(I32).rearrange("p (u j) -> p u j", u=POOL_PAGES)
+            nc.sync.dma_start(dst[:, :, cols], src[:, :, cols])
         nc.sync.dma_start(q_codes[:].bitcast(I32), q_words[0].rearrange("o p q r -> p o (q r)").bitcast(I32))
         nc.scalar.dma_start(vs_head[:, 0:8], vs[:, 0:8])
         nc.scalar.dma_start(staged[0:32, q_cols].bitcast(I32), q_scales[0].rearrange("o f q -> f o q").bitcast(I32))
@@ -107,24 +111,30 @@ def tile_attend_pkv4q_sigm_gate_kernel(
             nc.sync.dma_start(v_plane[32 * quad : 32 * quad + 4, :].bitcast(I32), rows.bitcast(I32))
         gate = own([NQ, DV], F32, "gate")
         nc.scalar.activation(gate[:], og_sb[:], SIGMOID)
+        k_codes = [own([P, PASSES, 2 * PAGE], U8, f"k_codes{c}") for c in range(PAGES)]
+
+        def gather(c, h, tag):
+            got = own([P, PAGE // 2], U32, f"k_got{c}{h}", tag=tag)
+            nc.vector.tensor_copy(got[:], k_pool[h][:].indirect(slots[:, 32 * c + 16 * h : 32 * c + 16 * (h + 1)]))
+            return got
+
+        def part(c, h, got, ts):
+            src = got[:].bitcast(U16).rearrange("p (m t o) -> p o m t", t=4, o=PASSES)
+            dst = k_codes[c][:].bitcast(U16).rearrange("p o (t m) -> p o m t", t=4)
+            nc.vector.tensor_copy(dst[:, :, 64 * h : 64 * (h + 1), ts], src[:, :, :, ts])
+
+        first = [gather(c, 0, f"first{c}") for c in range(PAGES)]
         for c in range(PAGES):
-            k_got = []
-            for h in range(2):
-                half = held.tile([P, PAGE // 2], U32, name=f"k_got{c}{h}", tag="k_got", bufs=2, align_bytes=64)
-                nc.vector.tensor_copy(half[:], k_pool[:].indirect(slots[:, 32 * c + 16 * h : 32 * c + 16 * (h + 1)]))
-                k_got.append(half)
-            k_codes = own([P, PASSES, 2 * PAGE], U8, f"k_codes{c}")
-            dst = k_codes[:].bitcast(U16).rearrange("p o (t m) -> p o m t", t=4)
-            for h in range(2):
-                src = k_got[h][:].bitcast(U16).rearrange("p (m t o) -> p o m t", t=4, o=PASSES)
-                last = c == PAGES - 1 and h == 1
-                for ts in [slice(t, t + 1) for t in range(4)] if last else [slice(0, 4)]:
-                    nc.vector.tensor_copy(dst[:, :, 64 * h : 64 * (h + 1), ts], src[:, :, :, ts])
+            part(c, 0, first[c], slice(0, 4))
+        for c in range(PAGES):
+            got = gather(c, 1, "second")
+            for a in range(2):
+                part(c, 1, got, slice(2 * a, 2 * a + 2))
             for t in range(4):
                 for o in range(PASSES):
                     nc.tensor.matmul_mx(
                         out=scores[2 * c + t // 2][:, t % 2, :],
-                        lhsT=k_codes[:, o, 256 * t : 256 * (t + 1)].bitcast(FP4X4),
+                        lhsT=k_codes[c][:, o, 256 * t : 256 * (t + 1)].bitcast(FP4X4),
                         lhsT_scale=planes[o][:, c * PAGE + P * t : c * PAGE + P * (t + 1)],
                         rhs=q_codes[:, o, :].bitcast(FP8X4),
                         rhs_scale=planes[o][:, q_cols],
@@ -132,7 +142,7 @@ def tile_attend_pkv4q_sigm_gate_kernel(
                         stop=(o == PASSES - 1),
                     )
 
-        v_got = held.tile([P, PAGES * DV], U32, name="v_got", tag="k_got", bufs=2, align_bytes=64)
+        v_got = own([P, PAGES * DV], U32, "v_got")
         nc.vector.tensor_copy(v_got[:], v_pool[:].indirect(vcols[:]))
 
 

@@ -63,13 +63,13 @@ def tile_attend_pkv4q_sigm_gate_kernel(
             src = k_words[0].rearrange("p t b -> p (t b)").bitcast(I32).rearrange("p (u j) -> p u j", u=POOL_PAGES)
             dst = k_pool[h][:].bitcast(I32).rearrange("p (u j) -> p u j", u=POOL_PAGES)
             nc.sync.dma_start(dst[:, :, cols], src[:, :, cols])
-        nc.sync.dma_start(q_codes[:].bitcast(I32), q_words[0].rearrange("o p q r -> p o (q r)").bitcast(I32))
-        nc.scalar.dma_start(vs_head[:, 0:8], vs[:, 0:8])
-        nc.scalar.dma_start(staged[0:32, q_cols].bitcast(I32), q_scales[0].rearrange("o f q -> f o q").bitcast(I32))
-        nc.scalar.dma_start(
+        nc.sync.dma_start(
             vsc_pool[P - 16 : P, :].bitcast(I32).rearrange("f (u e) -> f u e", u=POOL_PAGES),
             v_scales.rearrange("u f e -> f u e").bitcast(I32),
         )
+        nc.sync.dma_start(q_codes[:].bitcast(I32), q_words[0].rearrange("o p q r -> p o (q r)").bitcast(I32))
+        nc.scalar.dma_start(vs_head[:, 0:8], vs[:, 0:8])
+        nc.scalar.dma_start(staged[0:32, q_cols].bitcast(I32), q_scales[0].rearrange("o f q -> f o q").bitcast(I32))
         nc.scalar.dma_start(vs_pool[P - 1 : P, :], vs[0:1, :])
 
         nc.vector.memset(vsc_pool[0 : P - 16, :].bitcast(I32), 0)
@@ -88,16 +88,14 @@ def tile_attend_pkv4q_sigm_gate_kernel(
                 staged[:, c * PAGE : (c + 1) * PAGE].rearrange("p (t m) -> p t m", t=4),
                 ks_got[:, c, :].rearrange("p (m t) -> p t m", t=4),
             )
-        vsc_got = own([P, PAGES * DV], U8, "vsc_got", tag="ks_got")
-        nc.vector.tensor_copy(vsc_got[:], vsc_pool[:].indirect(vcols[:]))
         for quad in (0, 2, 1, 3):
             nc.sync.dma_start(both[32 * quad : 32 * quad + 4].bitcast(I32), staged[8 * quad : 8 * quad + 8, :].bitcast(I32))
-        nc.sync.dma_start(og_sb[:], og[0])
 
         nc.sync.dma_start(
             v_pool[:].bitcast(I32).rearrange("p (u e) -> p u e", u=POOL_PAGES),
             v_words.rearrange("u p e r -> p u (e r)").bitcast(I32),
         )
+        nc.sync.dma_start(og_sb[:], og[0])
         vs_col = [own([P, 4], F32, f"vs_col{c}") for c in range(PAGES)]
 
         scores = [psum.tile([P, 2, NQ], F32, name=f"scores{b}", tag=f"bank{b}") for b in range(2 * PAGES)]
@@ -106,9 +104,6 @@ def tile_attend_pkv4q_sigm_gate_kernel(
             nc.scalar.activation(vs_got[:, c * PAGE : (c + 1) * PAGE], vs_pool[:].indirect(slots[:, 32 * c : 32 * (c + 1)]), COPY)
             row = vs_got[P - 1 : P, c * PAGE : (c + 1) * PAGE]
             nc.sync.dma_start(vs_col[c][:], row.rearrange("p (m t) -> p m t", t=4))
-        for quad in range(4):
-            rows = vsc_got[P - 16 + 4 * quad : P - 12 + 4 * quad, :]
-            nc.sync.dma_start(v_plane[32 * quad : 32 * quad + 4, :].bitcast(I32), rows.bitcast(I32))
         gate = own([NQ, DV], F32, "gate")
         nc.scalar.activation(gate[:], og_sb[:], SIGMOID)
         k_codes = [own([P, PASSES, 2 * PAGE], U8, f"k_codes{c}") for c in range(PAGES)]
@@ -130,6 +125,12 @@ def tile_attend_pkv4q_sigm_gate_kernel(
             got = gather(c, 1, "second")
             for a in range(2):
                 part(c, 1, got, slice(2 * a, 2 * a + 2))
+            if c == 0:
+                vsc_got = own([P, PAGES * DV], U8, "vsc_got")
+                nc.vector.tensor_copy(vsc_got[:], vsc_pool[:].indirect(vcols[:]))
+                for quad in range(4):
+                    rows = vsc_got[P - 16 + 4 * quad : P - 12 + 4 * quad, :]
+                    nc.sync.dma_start(v_plane[32 * quad : 32 * quad + 4, :].bitcast(I32), rows.bitcast(I32))
             for t in range(4):
                 for o in range(PASSES):
                     nc.tensor.matmul_mx(

@@ -1,6 +1,7 @@
 from contextlib import ExitStack
 
 import concourse.mybir as mybir
+from concourse.masks import make_identity
 
 N, T, D, DV, NQ = 1024, 4096, 1024, 128, 128
 P = 128
@@ -9,7 +10,8 @@ PAGES = N // PAGE
 PASSES = D // 512
 POOL_PAGES = T // PAGE
 HALF = NQ // 2
-SPLIT = 1280
+QUARTER = PAGE // 4
+SHIFT = PAGE - QUARTER
 
 FLOPS = 2 * NQ * N * (D + DV)
 BYTES = P * T * 4 + 32 * T + POOL_PAGES * (P * DV * 4 + 16 * DV) + PASSES * (P * NQ * 4 + 16 * NQ) + T * 4 + 2 * NQ * DV * 4 + P * (N + PAGES * DV) // 8
@@ -42,8 +44,9 @@ def tile_attend_pkv4q_sigm_gate_kernel(
         slots = lists.tile([P, N // 16], U16, name="slots")
         vcols = lists.tile([P, PAGES * DV // 16], U16, name="vcols")
         ks_pool = own([P, T], U8, "ks_pool")
-        vs_pool = own([P, T], F32, "vs_pool")
-        vs_head = own([P, 8], F32, "vs_head")
+        vs_rows = own([P, PAGE], F32, "vs_rows")
+        vs_pool = own([P, SHIFT + T], F32, "vs_pool")
+        ident = own([P, P], F32, "ident")
         og_sb = own([P, DV], F32, "og_sb")
         k_pool = [own([P, T], U32, f"k_pool{h}") for h in range(2)]
         q_codes = own([P, PASSES, NQ], U32, "q_codes")
@@ -63,22 +66,28 @@ def tile_attend_pkv4q_sigm_gate_kernel(
             src = k_words[0].rearrange("p t b -> p (t b)").bitcast(I32).rearrange("p (u j) -> p u j", u=POOL_PAGES)
             dst = k_pool[h][:].bitcast(I32).rearrange("p (u j) -> p u j", u=POOL_PAGES)
             nc.sync.dma_start(dst[:, :, cols], src[:, :, cols])
-        nc.sync.dma_start(
+        nc.sync.dma_start(q_codes[:].bitcast(I32), q_words[0].rearrange("o p q r -> p o (q r)").bitcast(I32))
+        nc.scalar.dma_start(vs_rows[P - POOL_PAGES : P, :], vs[0].rearrange("(u j) -> u j", u=POOL_PAGES))
+        nc.scalar.dma_start(
             vsc_pool[P - 16 : P, :].bitcast(I32).rearrange("f (u e) -> f u e", u=POOL_PAGES),
             v_scales.rearrange("u f e -> f u e").bitcast(I32),
         )
-        nc.sync.dma_start(q_codes[:].bitcast(I32), q_words[0].rearrange("o p q r -> p o (q r)").bitcast(I32))
-        nc.scalar.dma_start(vs_head[:, 0:8], vs[:, 0:8])
         nc.scalar.dma_start(staged[0:32, q_cols].bitcast(I32), q_scales[0].rearrange("o f q -> f o q").bitcast(I32))
-        nc.scalar.dma_start(vs_pool[P - 1 : P, :], vs[0:1, :])
 
-        nc.vector.memset(vsc_pool[0 : P - 16, :].bitcast(I32), 0)
+        make_identity(nc, ident[:])
+        nc.vector.memset(vs_rows[0 : P - POOL_PAGES, :], 0.0)
         nc.vector.memset(ks_pool[32:64, :].bitcast(I32), 0)
         nc.vector.memset(ks_pool[64:P, :].bitcast(I32), 0)
-        nc.vector.memset(vs_pool[0 : P - 1, 0:SPLIT], 0.0)
-        nc.vector.memset(both[:].rearrange("p o c -> p (o c)").bitcast(I32), 0)
-        nc.vector.memset(v_plane[:].bitcast(I32), 0)
-        nc.scalar.copy(vs_pool[0 : P - 1, SPLIT:T], vs_head[0 : P - 1, 0:1].to_broadcast([P - 1, T - SPLIT]))
+        nc.vector.memset(vsc_pool[0 : P - 16, :].bitcast(I32), 0)
+
+        turned = psum.tile([P, 4, P], F32, name="turned")
+        for t in range(4):
+            nc.tensor.transpose(turned[:, t, :], vs_rows[:, t:PAGE:4], ident[:])
+        nc.scalar.activation(
+            vs_pool[:, SHIFT:].rearrange("p (u j) -> p u j", u=POOL_PAGES)[:, :, 0:QUARTER].rearrange("p u (i t) -> p u i t", t=4),
+            turned[:, :, P - POOL_PAGES : P].rearrange("p t (u o) -> p u o t", o=1).to_broadcast([P, POOL_PAGES, QUARTER // 4, 4]),
+            COPY,
+        )
 
         ks_got = own([P, PAGES, PAGE], U8, "ks_got")
         for c in range(PAGES):
@@ -96,14 +105,14 @@ def tile_attend_pkv4q_sigm_gate_kernel(
             v_words.rearrange("u p e r -> p u (e r)").bitcast(I32),
         )
         nc.sync.dma_start(og_sb[:], og[0])
-        vs_col = [own([P, 4], F32, f"vs_col{c}") for c in range(PAGES)]
 
         scores = [psum.tile([P, 2, NQ], F32, name=f"scores{b}", tag=f"bank{b}") for b in range(2 * PAGES)]
-        vs_got = own([P, N], F32, "vs_got")
+        factor = own([P, PAGES, PAGE], F32, "factor")
         for c in range(PAGES):
-            nc.scalar.activation(vs_got[:, c * PAGE : (c + 1) * PAGE], vs_pool[:].indirect(slots[:, 32 * c : 32 * (c + 1)]), COPY)
-            row = vs_got[P - 1 : P, c * PAGE : (c + 1) * PAGE]
-            nc.sync.dma_start(vs_col[c][:], row.rearrange("p (m t) -> p m t", t=4))
+            for k in range(4):
+                window = vs_pool[:, SHIFT - QUARTER * k : SHIFT - QUARTER * k + T]
+                offsets = slots[:, 32 * c + 8 * k : 32 * c + 8 * (k + 1)]
+                nc.scalar.activation(factor[:, c, QUARTER * k : QUARTER * (k + 1)], window.indirect(offsets), COPY)
         gate = own([NQ, DV], F32, "gate")
         nc.scalar.activation(gate[:], og_sb[:], SIGMOID)
         k_codes = [own([P, PASSES, 2 * PAGE], U8, f"k_codes{c}") for c in range(PAGES)]
@@ -121,16 +130,15 @@ def tile_attend_pkv4q_sigm_gate_kernel(
         first = [gather(c, 0, f"first{c}") for c in range(PAGES)]
         for c in range(PAGES):
             part(c, 0, first[c], slice(0, 4))
+        vsc_got = own([P, PAGES * DV], U8, "vsc_got", tag="first0")
+        nc.vector.tensor_copy(vsc_got[:], vsc_pool[:].indirect(vcols[:]))
+        for quad in range(4):
+            rows = vsc_got[P - 16 + 4 * quad : P - 12 + 4 * quad, :]
+            nc.sync.dma_start(v_plane[32 * quad : 32 * quad + 4, :].bitcast(I32), rows.bitcast(I32))
         for c in range(PAGES):
             got = gather(c, 1, "second")
             for a in range(2):
                 part(c, 1, got, slice(2 * a, 2 * a + 2))
-            if c == 0:
-                vsc_got = own([P, PAGES * DV], U8, "vsc_got")
-                nc.vector.tensor_copy(vsc_got[:], vsc_pool[:].indirect(vcols[:]))
-                for quad in range(4):
-                    rows = vsc_got[P - 16 + 4 * quad : P - 12 + 4 * quad, :]
-                    nc.sync.dma_start(v_plane[32 * quad : 32 * quad + 4, :].bitcast(I32), rows.bitcast(I32))
             for t in range(4):
                 for o in range(PASSES):
                     nc.tensor.matmul_mx(
@@ -156,11 +164,10 @@ def tile_attend_pkv4q_sigm_gate_kernel(
             nc.scalar.activation(prob[:, 0, :, :], scores[2 * c][:].rearrange("p t q -> p q t"), SIGMOID)
             for qs in halves:
                 nc.scalar.activation(prob[:, 1, qs, :], scores[2 * c + 1][:, :, qs].rearrange("p t q -> p q t"), SIGMOID)
-                factor = vs_col[c][:].rearrange("p (o a t) -> p o a t", o=1, a=2)
                 nc.vector.tensor_tensor(
                     w[c][:, qs, :].rearrange("p q (a t) -> p q a t", a=2),
                     prob[:, :, qs, :].rearrange("p a q t -> p q a t"),
-                    factor.to_broadcast([P, qs.stop - qs.start, 2, 2]),
+                    factor[:, c, :].rearrange("p (q a t) -> p q a t", a=2, t=2)[:, qs],
                     MULT,
                 )
         for c in range(PAGES):

@@ -60,18 +60,18 @@ def tile_attend_pkv4q_sigm_gate_kernel(
 
         nc.sync.dma_start(ks_pool[0:32, :].bitcast(I32), k_scales.rearrange("o f t -> f o t").bitcast(I32))
         nc.sync.dma_start(slots[:], offs)
-        nc.sync.dma_start(vcols[:], voffs)
         for h in range(2):
             cols = slice(h * PAGE // 2, (h + 1) * PAGE // 2)
             src = k_words[0].rearrange("p t b -> p (t b)").bitcast(I32).rearrange("p (u j) -> p u j", u=POOL_PAGES)
             dst = k_pool[h][:].bitcast(I32).rearrange("p (u j) -> p u j", u=POOL_PAGES)
             nc.sync.dma_start(dst[:, :, cols], src[:, :, cols])
-        nc.sync.dma_start(q_codes[:].bitcast(I32), q_words[0].rearrange("o p q r -> p o (q r)").bitcast(I32))
-        nc.scalar.dma_start(vs_rows[P - POOL_PAGES : P, :], vs[0].rearrange("(u j) -> u j", u=POOL_PAGES))
-        nc.scalar.dma_start(
+        nc.sync.dma_start(vcols[:], voffs)
+        nc.sync.dma_start(
             vsc_pool[P - 16 : P, :].bitcast(I32).rearrange("f (u e) -> f u e", u=POOL_PAGES),
             v_scales.rearrange("u f e -> f u e").bitcast(I32),
         )
+        nc.sync.dma_start(q_codes[:].bitcast(I32), q_words[0].rearrange("o p q r -> p o (q r)").bitcast(I32))
+        nc.scalar.dma_start(vs_rows[P - POOL_PAGES : P, :], vs[0].rearrange("(u j) -> u j", u=POOL_PAGES))
         nc.scalar.dma_start(staged[0:32, q_cols].bitcast(I32), q_scales[0].rearrange("o f q -> f o q").bitcast(I32))
 
         make_identity(nc, ident[:])
@@ -130,15 +130,16 @@ def tile_attend_pkv4q_sigm_gate_kernel(
         first = [gather(c, 0, f"first{c}") for c in range(PAGES)]
         for c in range(PAGES):
             part(c, 0, first[c], slice(0, 4))
-        vsc_got = own([P, PAGES * DV], U8, "vsc_got", tag="first0")
-        nc.vector.tensor_copy(vsc_got[:], vsc_pool[:].indirect(vcols[:]))
-        for quad in range(4):
-            rows = vsc_got[P - 16 + 4 * quad : P - 12 + 4 * quad, :]
-            nc.sync.dma_start(v_plane[32 * quad : 32 * quad + 4, :].bitcast(I32), rows.bitcast(I32))
         for c in range(PAGES):
             got = gather(c, 1, "second")
             for a in range(2):
                 part(c, 1, got, slice(2 * a, 2 * a + 2))
+            if c == 0:
+                vsc_got = own([P, PAGES * DV], U8, "vsc_got")
+                nc.vector.tensor_copy(vsc_got[:], vsc_pool[:].indirect(vcols[:]))
+                for quad in range(4):
+                    rows = vsc_got[P - 16 + 4 * quad : P - 12 + 4 * quad, :]
+                    nc.sync.dma_start(v_plane[32 * quad : 32 * quad + 4, :].bitcast(I32), rows.bitcast(I32))
             for t in range(4):
                 for o in range(PASSES):
                     nc.tensor.matmul_mx(

@@ -115,7 +115,7 @@ def tile_attend_pkv4q_sigm_gate_kernel(
                 nc.scalar.activation(factor[:, c, QUARTER * k : QUARTER * (k + 1)], window.indirect(offsets), COPY)
         gate = own([NQ, DV], F32, "gate")
         nc.scalar.activation(gate[:], og_sb[:], SIGMOID)
-        k_codes = [own([P, PASSES, 2 * PAGE], U8, f"k_codes{c}") for c in range(PAGES)]
+        k_codes = [own([P, PASSES, 2 * PAGE], U8, f"k_codes{c}", tag=("k_codes0", "staged")[c]) for c in range(PAGES)]
 
         def gather(c, h, tag):
             got = own([P, PAGE // 2], U32, f"k_got{c}{h}", tag=tag)
@@ -134,8 +134,8 @@ def tile_attend_pkv4q_sigm_gate_kernel(
             got = gather(c, 1, "second")
             for a in range(2):
                 part(c, 1, got, slice(2 * a, 2 * a + 2))
-            if c == 0:
-                vsc_got = own([P, PAGES * DV], U8, "vsc_got")
+            if c == 1:
+                vsc_got = own([P, PAGES * DV], U8, "vsc_got", tag="first1")
                 nc.vector.tensor_copy(vsc_got[:], vsc_pool[:].indirect(vcols[:]))
                 for quad in range(4):
                     rows = vsc_got[P - 16 + 4 * quad : P - 12 + 4 * quad, :]

from contextlib import ExitStack

import concourse.mybir as mybir
from concourse.masks import make_identity

N, T, D, DV, NQ = 1024, 4096, 1024, 128, 128
P = 128
PAGE = 512
PAGES = N // PAGE
PASSES = D // 512
POOL_PAGES = T // PAGE
HALF = NQ // 2
QUARTER = PAGE // 4
SHIFT = PAGE - QUARTER

FLOPS = 2 * NQ * N * (D + DV)
BYTES = P * T * 4 + 32 * T + POOL_PAGES * (P * DV * 4 + 16 * DV) + PASSES * (P * NQ * 4 + 16 * NQ) + T * 4 + 2 * NQ * DV * 4 + P * (N + PAGES * DV) // 8

F32 = mybir.dt.float32
BF16 = mybir.dt.bfloat16
I32 = mybir.dt.int32
U32 = mybir.dt.uint32
U16 = mybir.dt.uint16
U8 = mybir.dt.uint8
FP8X4 = mybir.dt.float8_e4m3fn_x4
FP4X4 = mybir.dt.float4_e2m1fn_x4
MULT = mybir.AluOpType.mult
SIGMOID = mybir.ActivationFunctionType.Sigmoid
COPY = mybir.ActivationFunctionType.Copy


def tile_attend_pkv4q_sigm_gate_kernel(
    tc, q_words, q_scales, k_words, k_scales, v_words, v_scales, vs, og, offs, voffs, out
):
    nc = tc.nc
    with ExitStack() as ctx:
        lists = ctx.enter_context(tc.tile_pool(name="lists", bufs=1))
        held = ctx.enter_context(tc.tile_pool(name="held", bufs=1))
        psum = ctx.enter_context(tc.psum_pool(name="psum", bufs=1))

        def own(shape, dtype, name, tag=None):
            return held.tile(shape, dtype, name=name, tag=tag or name, align_bytes=64)

        slots = lists.tile([P, N // 16], U16, name="slots")
        vcols = lists.tile([P, PAGES * DV // 16], U16, name="vcols")
        ks_pool = own([P, T], U8, "ks_pool")
        vs_rows = own([P, PAGE], F32, "vs_rows")
        vs_pool = own([P, SHIFT + T], F32, "vs_pool")
        ident = own([P, P], F32, "ident")
        og_sb = own([P, DV], F32, "og_sb")
        k_pool = [own([P, T], U32, f"k_pool{h}") for h in range(2)]
        q_codes = own([P, PASSES, NQ], U32, "q_codes")
        staged = own([P, N + NQ], U8, "staged")
        both = own([P, PASSES, N + NQ], U8, "both")
        v_plane = own([P, PAGES * DV], U8, "v_plane")
        planes = [both[:, o, :] for o in range(PASSES)]
        q_cols = slice(N, N + NQ)
        vsc_pool = own([P, POOL_PAGES * DV], U8, "vsc_pool")
        v_pool = own([P, POOL_PAGES * DV], U32, "v_pool")

        nc.sync.dma_start(ks_pool[0:32, :].bitcast(I32), k_scales.rearrange("o f t -> f o t").bitcast(I32))
        nc.sync.dma_start(slots[:], offs)
        for h in range(2):
            cols = slice(h * PAGE // 2, (h + 1) * PAGE // 2)
            src = k_words[0].rearrange("p t b -> p (t b)").bitcast(I32).rearrange("p (u j) -> p u j", u=POOL_PAGES)
            dst = k_pool[h][:].bitcast(I32).rearrange("p (u j) -> p u j", u=POOL_PAGES)
            nc.sync.dma_start(dst[:, :, cols], src[:, :, cols])
        nc.sync.dma_start(vcols[:], voffs)
        nc.sync.dma_start(
            vsc_pool[P - 16 : P, :].bitcast(I32).rearrange("f (u e) -> f u e", u=POOL_PAGES),
            v_scales.rearrange("u f e -> f u e").bitcast(I32),
        )
        nc.sync.dma_start(q_codes[:].bitcast(I32), q_words[0].rearrange("o p q r -> p o (q r)").bitcast(I32))
        nc.scalar.dma_start(vs_rows[P - POOL_PAGES : P, :], vs[0].rearrange("(u j) -> u j", u=POOL_PAGES))
        nc.scalar.dma_start(staged[0:32, q_cols].bitcast(I32), q_scales[0].rearrange("o f q -> f o q").bitcast(I32))

        make_identity(nc, ident[:])
        nc.vector.memset(vs_rows[0 : P - POOL_PAGES, :], 0.0)
        nc.vector.memset(ks_pool[32:64, :].bitcast(I32), 0)
        nc.vector.memset(ks_pool[64:P, :].bitcast(I32), 0)
        nc.vector.memset(vsc_pool[0 : P - 16, :].bitcast(I32), 0)

        turned = psum.tile([P, 4, P], F32, name="turned")
        for t in range(4):
            nc.tensor.transpose(turned[:, t, :], vs_rows[:, t:PAGE:4], ident[:])
        nc.scalar.activation(
            vs_pool[:, SHIFT:].rearrange("p (u j) -> p u j", u=POOL_PAGES)[:, :, 0:QUARTER].rearrange("p u (i t) -> p u i t", t=4),
            turned[:, :, P - POOL_PAGES : P].rearrange("p t (u o) -> p u o t", o=1).to_broadcast([P, POOL_PAGES, QUARTER // 4, 4]),
            COPY,
        )

        ks_got = own([P, PAGES, PAGE], U8, "ks_got")
        for c in range(PAGES):
            nc.vector.tensor_copy(ks_got[:, c, :], ks_pool[:].indirect(slots[:, 32 * c : 32 * (c + 1)]))
        for c in range(PAGES):
            nc.vector.tensor_copy(
                staged[:, c * PAGE : (c + 1) * PAGE].rearrange("p (t m) -> p t m", t=4),
                ks_got[:, c, :].rearrange("p (m t) -> p t m", t=4),
            )
        for quad in (0, 2, 1, 3):
            nc.sync.dma_start(both[32 * quad : 32 * quad + 4].bitcast(I32), staged[8 * quad : 8 * quad + 8, :].bitcast(I32))

        nc.sync.dma_start(
            v_pool[:].bitcast(I32).rearrange("p (u e) -> p u e", u=POOL_PAGES),
            v_words.rearrange("u p e r -> p u (e r)").bitcast(I32),
        )
        nc.sync.dma_start(og_sb[:], og[0])

        scores = [psum.tile([P, 2, NQ], F32, name=f"scores{b}", tag=f"bank{b}") for b in range(2 * PAGES)]
        factor = own([P, PAGES, PAGE], F32, "factor")
        for c in range(PAGES):
            for k in range(4):
                window = vs_pool[:, SHIFT - QUARTER * k : SHIFT - QUARTER * k + T]
                offsets = slots[:, 32 * c + 8 * k : 32 * c + 8 * (k + 1)]
                nc.scalar.activation(factor[:, c, QUARTER * k : QUARTER * (k + 1)], window.indirect(offsets), COPY)
        gate = own([NQ, DV], F32, "gate")
        nc.scalar.activation(gate[:], og_sb[:], SIGMOID)
        k_codes = [own([P, PASSES, 2 * PAGE], U8, f"k_codes{c}", tag=("k_codes0", "staged")[c]) for c in range(PAGES)]

        def gather(c, h, tag):
            got = own([P, PAGE // 2], U32, f"k_got{c}{h}", tag=tag)
            nc.vector.tensor_copy(got[:], k_pool[h][:].indirect(slots[:, 32 * c + 16 * h : 32 * c + 16 * (h + 1)]))
            return got

        def part(c, h, got, ts):
            src = got[:].bitcast(U16).rearrange("p (m t o) -> p o m t", t=4, o=PASSES)
            dst = k_codes[c][:].bitcast(U16).rearrange("p o (t m) -> p o m t", t=4)
            nc.vector.tensor_copy(dst[:, :, 64 * h : 64 * (h + 1), ts], src[:, :, :, ts])

        first = [gather(c, 0, f"first{c}") for c in range(PAGES)]
        for c in range(PAGES):
            part(c, 0, first[c], slice(0, 4))
        for c in range(PAGES):
            got = gather(c, 1, "second")
            for a in range(2):
                part(c, 1, got, slice(2 * a, 2 * a + 2))
            if c == 1:
                vsc_got = own([P, PAGES * DV], U8, "vsc_got", tag="first1")
                nc.vector.tensor_copy(vsc_got[:], vsc_pool[:].indirect(vcols[:]))
                for quad in range(4):
                    rows = vsc_got[P - 16 + 4 * quad : P - 12 + 4 * quad, :]
                    nc.sync.dma_start(v_plane[32 * quad : 32 * quad + 4, :].bitcast(I32), rows.bitcast(I32))
            for t in range(4):
                for o in range(PASSES):
                    nc.tensor.matmul_mx(
                        out=scores[2 * c + t // 2][:, t % 2, :],
                        lhsT=k_codes[c][:, o, 256 * t : 256 * (t + 1)].bitcast(FP4X4),
                        lhsT_scale=planes[o][:, c * PAGE + P * t : c * PAGE + P * (t + 1)],
                        rhs=q_codes[:, o, :].bitcast(FP8X4),
                        rhs_scale=planes[o][:, q_cols],
                        start=(o == 0),
                        stop=(o == PASSES - 1),
                    )

        v_got = own([P, PAGES * DV], U32, "v_got")
        nc.vector.tensor_copy(v_got[:], v_pool[:].indirect(vcols[:]))


        acc = psum.tile([NQ, DV], F32, name="acc")
        halves = [slice(h * HALF, (h + 1) * HALF) for h in range(2)]
        pieces = ([slice(0, NQ)], halves)
        w = [own([P, NQ, 4], BF16, f"w{c}") for c in range(PAGES)]
        for c in range(PAGES):
            prob = own([P, 2, NQ, 2], F32, f"prob{c}")
            nc.scalar.activation(prob[:, 0, :, :], scores[2 * c][:].rearrange("p t q -> p q t"), SIGMOID)
            for qs in halves:
                nc.scalar.activation(prob[:, 1, qs, :], scores[2 * c + 1][:, :, qs].rearrange("p t q -> p q t"), SIGMOID)
                nc.vector.tensor_tensor(
                    w[c][:, qs, :].rearrange("p q (a t) -> p q a t", a=2),
                    prob[:, :, qs, :].rearrange("p a q t -> p q a t"),
                    factor[:, c, :].rearrange("p (q a t) -> p q a t", a=2, t=2)[:, qs],
                    MULT,
                )
        for c in range(PAGES):
            w_codes = own([P, NQ], U32, f"w_codes{c}")
            w_plane = own([P, NQ], U8, f"w_plane{c}")
            for qs in pieces[c]:
                nc.vector.quantize_mx(
                    out=w_codes[:, qs].bitcast(FP8X4),
                    scales=w_plane[:, qs],
                    in_=w[c][:, qs, :].rearrange("p q t -> p (q t)"),
                )
            nc.tensor.matmul_mx(
                out=acc[:],
                lhsT=w_codes[:].bitcast(FP8X4),
                lhsT_scale=w_plane[:],
                rhs=v_got[:, c * DV : (c + 1) * DV].bitcast(FP8X4),
                rhs_scale=v_plane[:, c * DV : (c + 1) * DV],
                start=(c == 0),
                stop=(c == PAGES - 1),
            )

        result = own([NQ, DV], F32, "result")
        nc.vector.scalar_tensor_tensor(result[:], acc[:], 1.0 / 16.0, gate[:], MULT, MULT)
        nc.sync.dma_start(out[0], result[:])
